import numpy as np
import ml_dtypes


def mxq(x, axis, fmt="e4m3"):
    dtype, down = {"e4m3": (ml_dtypes.float8_e4m3fn, 7), "e5m2": (ml_dtypes.float8_e5m2, 14)}[fmt]
    v = np.moveaxis(np.asarray(x, np.float32).astype(ml_dtypes.bfloat16).astype(np.float64), axis, -1)
    blocks = v.reshape(v.shape[:-1] + (-1, 32))
    amax = np.abs(blocks).max(-1, keepdims=True)
    byte = np.maximum(np.where(amax > 0, np.frexp(amax)[1] - 1 + 127, 0) - down, 1)
    scale = np.exp2(byte - 127.0)
    codes = (blocks / scale).astype(np.float32).astype(dtype).astype(np.float64)
    return np.moveaxis((codes * scale).reshape(v.shape), -1, axis)


WIDE = False


def mx_kscale(k):
    if not WIDE:
        return np.ones(k)
    levels = np.array([10, -10, 5, -5, 0])
    if k % 512:
        return np.exp2(np.random.permutation(np.resize(levels, k // 32))).repeat(32)
    a = np.empty((k // 512, 16))
    for p in range(k // 512):
        a[p, :8] = np.random.permutation(np.resize(levels, 8))
        for g in range(8):
            far = levels[np.abs(levels - a[p, g]) >= 10]
            a[p, g + 8] = far[np.random.randint(len(far))]
    return np.exp2(a.ravel()).repeat(32)


def f64(x):
    return np.asarray(x).astype(np.float64)


def striped(idx):
    return np.tile(idx.reshape(-1, 16).T, (8, 1)).astype(np.uint16)


def unstriped(offs):
    return offs[:16].T.reshape(-1).astype(np.int64)


def pack_weight(w):
    k, n = w.shape
    w = f64(np.asarray(w, np.float32).astype(ml_dtypes.bfloat16)).reshape(k // 32, 32, n)
    amax = np.abs(w).max(1)
    byte = np.clip(np.where(amax > 0, np.frexp(amax)[1] - 1 + 127 - 7, 1), 1, 254)
    scaled = (w * np.exp2(127.0 - byte)[:, None, :]).reshape(k, n).astype(np.float32)
    words = np.ascontiguousarray(scaled.reshape(k // 512, 128, 4, n).transpose(0, 1, 3, 2)).astype(ml_dtypes.float8_e4m3fn).view(np.uint8)
    return words, np.ascontiguousarray(byte.astype(np.uint8).reshape(k // 512, 16, n))


def unpack_weight(words, scales):
    g, p, n, _ = words.shape
    vals = np.ascontiguousarray(words).view(ml_dtypes.float8_e4m3fn).astype(np.float64) * np.repeat(np.exp2(scales.astype(np.float64) - 127.0), 8, axis=1)[..., None]
    return vals.transpose(0, 1, 3, 2).reshape(g * 512, n)


K, T, S, V = 512, 2048, 512, 512
P = 2 ** 7


def setup_inputs():
    n = np.random.standard_normal
    s = mx_kscale(K)[:, None]
    packed_xT = pack_weight(n((K, T)) * s)
    packed_eT = pack_weight(n((K, T)) * s)
    return {
        "x_words": packed_xT[0],
        "x_scales": packed_xT[1],
        "e_words": packed_eT[0],
        "e_scales": packed_eT[1],
        "hr": (n((K, V)) / np.sqrt(K) / s).astype(np.float32),
        "hi": (n((K, V)) / np.sqrt(K) / s).astype(np.float32),
        "inv": (np.tile(np.random.uniform(0.5, 1.5, T), (P, 1))).astype(np.float32),
        "offs": striped(np.random.permutation(T)[:S]),
    }


def reference(x_words, x_scales, e_words, e_scales, hr, hi, inv, offs):
    hrq = mxq(f64(hr), 0, "e4m3")
    xq = unpack_weight(x_words, x_scales)[:, unstriped(offs)]
    hiq = mxq(f64(hi), 0, "e4m3")
    e_offs = unpack_weight(e_words, e_scales)[:, unstriped(offs)]
    re = hrq.T @ xq + hiq.T @ e_offs
    z = hrq.T @ e_offs
    im = (hiq.T @ xq) - z
    mm = ((re) ** 2 + (im) ** 2) * (f64(inv)[:1][:, unstriped(offs)])
    top = mm.max(axis=1, keepdims=True)
    rr = 6.0 * (mm / top)
    return rr * np.exp(rr - 6.0)

@@ -1,0 +1,197 @@
+import math
+from contextlib import ExitStack
+
+import concourse.mybir as mybir
+from concourse.masks import make_identity
+
+K, T, S, V = 512, 2048, 512, 512
+FLOPS = 4 * 2 * K * V * S
+BYTES = 2 * K * T + 2 * (K // 32) * T + 2 * K * V * 4 + T * 4 + 128 * (S // 16) * 2 + V * S * 4
+
+F32 = mybir.dt.float32
+BF16 = mybir.dt.bfloat16
+I32 = mybir.dt.int32
+U32 = mybir.dt.uint32
+U16 = mybir.dt.uint16
+U8 = mybir.dt.uint8
+FP8X4 = mybir.dt.float8_e4m3fn_x4
+ALU = mybir.AluOpType
+ACT = mybir.ActivationFunctionType
+
+P = 128
+PACK = 4
+HALF = V // 2
+ATOM_BLOCKS = S // P
+VOXEL_BLOCKS = V // P
+E_PLANE = 4
+EARLY_UNITS = 5
+VECTOR_UNIT = 2
+
+
+def tile_picked_ymrf_steep_p_kernel(tc, x_words, x_scales, e_words, e_scales, hr, hi, inv, offs, out):
+    nc = tc.nc
+    with ExitStack() as ctx:
+        held = ctx.enter_context(tc.tile_pool(name="held", bufs=1))
+        reused = ctx.enter_context(tc.tile_pool(name="reused", bufs=1))
+        psum = ctx.enter_context(tc.psum_pool(name="psum", bufs=1))
+
+        def bank(b):
+            return psum.tile([P, 512], F32, name="bank%d" % b, tag="bank%d" % b)
+
+        offsets = held.tile([P, S // 16], U16, name="offsets")
+        nc.sync.dma_start(offsets[:], offs)
+
+        hr_raw = held.tile([P, PACK, V], F32, name="hr_raw")
+        hi_raw = held.tile([P, PACK, V], F32, name="hi_raw")
+        x_table = held.tile([P, T], I32, name="x_table")
+        e_table = held.tile([P, T], I32, name="e_table")
+        x_scale_table = held.tile([P, T], U8, name="x_scale_table")
+        e_scale_table = held.tile([P, T], U8, name="e_scale_table")
+        inv_table = reused.tile([P, T], F32, name="inv_table", offset=0, align_bytes=64)
+        half = held.tile([P, ATOM_BLOCKS], F32, name="half")
+        warm = held.tile([P, 1], F32, name="warm")
+        identity = held.tile([P, P], F32, name="identity")
+        nc.gpsimd.memset(x_scale_table[:].bitcast(I32), 0)
+        nc.vector.memset(inv_table[:, 0:1280].bitcast(I32), 0)
+        nc.gpsimd.memset(inv_table[:, 1280:T].bitcast(I32), 0)
+        nc.vector.memset(half[:], 0.5)
+        nc.gpsimd.memset(e_scale_table[:].bitcast(I32), 0)
+        make_identity(nc, identity[:])
+        x_rows = x_scales[0].bitcast(I32).rearrange("(q r) c -> r q c", r=4)
+        e_rows = e_scales[0].bitcast(I32).rearrange("(q r) c -> r q c", r=4)
+        nc.sync.dma_start(hr_raw[:], hr.rearrange("(p j) t -> p j t", j=PACK))
+        for r in range(4):
+            nc.scalar.dma_start(x_scale_table[r:P:32, :].bitcast(I32), x_rows[r])
+        nc.scalar.dma_start(inv_table[0:1, :], inv[0:1, :])
+        nc.scalar.activation(warm[:], half[:, 0:1], ACT.Exp)
+        nc.sync.dma_start(e_scale_table[E_PLANE:P:32, :].bitcast(I32), e_rows[0])
+        nc.sync.dma_start(hi_raw[:], hi.rearrange("(p j) t -> p j t", j=PACK))
+        nc.sync.dma_start(x_table[:], x_words[0].rearrange("p n r -> p (n r)").bitcast(I32))
+        for r in range(1, 4):
+            nc.sync.dma_start(e_scale_table[E_PLANE + r : P : 32, :].bitcast(I32), e_rows[r])
+        nc.sync.dma_start(e_table[:], e_words[0].rearrange("p n r -> p (n r)").bitcast(I32))
+
+        x_scale = held.tile([P, S], U8, name="x_scale", align_bytes=64)
+        e_scale = held.tile([P, S], U8, name="e_scale", align_bytes=64)
+        inv_row = held.tile([P, S], F32, name="inv_row")
+        nc.vector.tensor_copy(x_scale[:], x_scale_table[:].indirect(offsets[:]))
+        nc.vector.tensor_copy(inv_row[:], inv_table[:].indirect(offsets[:]))
+
+        turned = bank(7)
+        for a in range(ATOM_BLOCKS):
+            nc.tensor.transpose(turned[:, a * P : (a + 1) * P], inv_row[:, a * P : (a + 1) * P], identity[:])
+        inv_col = held.tile([P, ATOM_BLOCKS], F32, name="inv_col")
+        root = held.tile([P, ATOM_BLOCKS], F32, name="root")
+        nc.scalar.copy(inv_col[:], turned[:, 0:S:P])
+        nc.gpsimd.tensor_tensor(root[:], inv_col[:], half[:], ALU.pow)
+
+        codes = [held.tile([P, 3 * HALF], U32, name="codes%d" % h, align_bytes=64) for h in range(2)]
+        scales = [
+            reused.tile([P, 3 * HALF], U8, name="scales%d" % h, offset=4096 + 1024 * h, align_bytes=64) for h in range(2)
+        ]
+
+        def interleave(raw, h, name):
+            grouped = held.tile([P, PACK * HALF], BF16, name=name, align_bytes=64)
+            nc.scalar.copy(
+                grouped[:].rearrange("p (c i j) -> p c j i", i=4, j=PACK),
+                raw[:, :, h * HALF : (h + 1) * HALF].rearrange("p j (c i) -> p c j i", i=4),
+            )
+            return grouped
+
+        def quantise(grouped, h, slot):
+            cols = slice(slot * HALF, (slot + 1) * HALF)
+            nc.vector.quantize_mx(out=codes[h][:, cols].bitcast(FP8X4), scales=scales[h][:, cols], in_=grouped[:])
+
+        for h in range(2):
+            plus = interleave(hr_raw, h, "hr_bf%d" % h)
+            minus = reused.tile([P, PACK * HALF], BF16, name="minus_hr_bf%d" % h, offset=2048 * h, align_bytes=64)
+            nc.vector.tensor_scalar(minus[:], plus[:], -1.0, None, ALU.mult)
+            quantise(plus, h, 0)
+            quantise(minus, h, 2)
+        for h in range(2):
+            quantise(interleave(hi_raw, h, "hi_bf%d" % h), h, 1)
+
+        def pick_words(table, name):
+            picked = []
+            for u in range(2):
+                words = held.tile([P, S // 2], U32, name="%s%d" % (name, u), align_bytes=64)
+                nc.vector.tensor_copy(words[:], table[:].bitcast(U32).indirect(offsets[:, u * 16 : (u + 1) * 16]))
+                picked.extend([words[:, 0:P], words[:, P : 2 * P]])
+            return picked
+
+        x_picked = pick_words(x_table, "x_picked")
+        nc.vector.tensor_copy(e_scale[:], e_scale_table[:].indirect(offsets[:]))
+        e_picked = pick_words(e_table, "e_picked")
+
+        def product_pass(target, h, a, table, start):
+            if table == "x":
+                words, plane, first = x_picked[a], x_scale[:, a * P : (a + 1) * P], 0
+            else:
+                words, plane, first = e_picked[a], e_scale[E_PLANE:P, a * P : (a + 1) * P], HALF
+            nc.tensor.matmul_mx(
+                out=target[:],
+                lhsT=words.bitcast(FP8X4),
+                lhsT_scale=plane,
+                rhs=codes[h][:, first : first + 2 * HALF].bitcast(FP8X4),
+                rhs_scale=scales[h][:, first : first + 2 * HALF],
+                start=start,
+                stop=not start,
+            )
+
+        units = [(h, a) for h in range(2) for a in range(ATOM_BLOCKS)]
+        products = {unit: bank(b) for b, unit in enumerate(units)}
+        squares = {}
+
+        def finish_unit(b):
+            h, a = units[b]
+            target = products[h, a]
+            product_pass(target, h, a, "e", b >= EARLY_UNITS)
+            if b >= EARLY_UNITS:
+                product_pass(target, h, a, "x", False)
+            squares[h, a] = held.tile([P, 2 * HALF], F32, name="squares%d_%d" % (h, a))
+            if b == VECTOR_UNIT:
+                scaled = held.tile([P, 2 * HALF], F32, name="scaled")
+                parts = [slice(0, HALF), slice(HALF, 2 * HALF)]
+                for cols in parts:
+                    nc.vector.tensor_scalar(scaled[:, cols], target[:, cols], root[:, a : a + 1], None, ALU.mult)
+                for cols in parts:
+                    nc.vector.tensor_tensor(squares[h, a][:, cols], scaled[:, cols], scaled[:, cols], ALU.mult)
+            else:
+                nc.scalar.activation(squares[h, a][:], target[:], ACT.Square, scale=root[:, a : a + 1])
+
+        def finish_block(v, match, pieces):
+            h, first = divmod(v * P, HALF)
+            for a in range(ATOM_BLOCKS):
+                for part in range(2):
+                    nc.tensor.matmul(
+                        match[:, a * P : (a + 1) * P],
+                        squares[h, a][:, part * HALF + first : part * HALF + first + P],
+                        identity[:],
+                        start=(part == 0),
+                        stop=(part == 1),
+                        is_transpose=True,
+                    )
+            sixth = held.tile([P, S], F32, name="sixth%d" % v)
+            top_sixth = held.tile([P, 1], F32, name="top_sixth%d" % v)
+            gain = held.tile([P, 1], F32, name="gain%d" % v)
+            weight = held.tile([P, S], F32, name="weight%d" % v)
+            result = held.tile([P, S], F32, name="result%d" % v)
+            nc.vector.tensor_scalar(sixth[:], match[:], 1.0 / 6.0, None, ALU.mult, ALU.max, accum_out=top_sixth[:])
+            nc.vector.reciprocal(gain[:], top_sixth[:])
+            width = S // pieces
+            for first_col in range(0, S, width):
+                cols = slice(first_col, first_col + width)
+                nc.scalar.activation(weight[:, cols], match[:, cols], ACT.Exp, bias=math.log(6.0) - 6.0, scale=gain[:])
+                nc.vector.scalar_tensor_tensor(result[:, cols], sixth[:, cols], gain[:], weight[:, cols], ALU.mult, ALU.mult)
+                nc.sync.dma_start(out[v * P : (v + 1) * P, cols], result[:, cols])
+
+        for h, a in units[:EARLY_UNITS]:
+            product_pass(products[h, a], h, a, "x", True)
+        for b in range(6):
+            finish_unit(b)
+        finish_block(0, bank(3), 1)
+        finish_block(1, bank(2), 1)
+        for b in range(6, 8):
+            finish_unit(b)
+        finish_block(2, bank(0), 1)
+        finish_block(3, bank(1), 2)

@@ -24,15 +24,14 @@ HALF = V // 2
 ATOM_BLOCKS = S // P
 VOXEL_BLOCKS = V // P
 E_PLANE = 4
-EARLY_UNITS = 5
-VECTOR_UNIT = 2
+EARLY_UNITS = 4
+WARM_PASSES = 6
 
 
 def tile_picked_ymrf_steep_p_kernel(tc, x_words, x_scales, e_words, e_scales, hr, hi, inv, offs, out):
     nc = tc.nc
     with ExitStack() as ctx:
         held = ctx.enter_context(tc.tile_pool(name="held", bufs=1))
-        reused = ctx.enter_context(tc.tile_pool(name="reused", bufs=1))
         psum = ctx.enter_context(tc.psum_pool(name="psum", bufs=1))
 
         def bank(b):
@@ -41,34 +40,34 @@ def tile_picked_ymrf_steep_p_kernel(tc, x_words, x_scales, e_words, e_scales, hr
         offsets = held.tile([P, S // 16], U16, name="offsets")
         nc.sync.dma_start(offsets[:], offs)
 
-        hr_raw = held.tile([P, PACK, V], F32, name="hr_raw")
-        hi_raw = held.tile([P, PACK, V], F32, name="hi_raw")
-        x_table = held.tile([P, T], I32, name="x_table")
-        e_table = held.tile([P, T], I32, name="e_table")
+        raw = held.tile([P, 2, PACK, V], F32, name="raw", tag="raw")
+        x_table = held.tile([P, T], I32, name="x_table", tag="x_table", align_bytes=64)
+        e_table = held.tile([P, T], I32, name="e_table", tag="e_table", align_bytes=64)
         x_scale_table = held.tile([P, T], U8, name="x_scale_table")
-        e_scale_table = held.tile([P, T], U8, name="e_scale_table")
-        inv_table = reused.tile([P, T], F32, name="inv_table", offset=0, align_bytes=64)
+        e_scale_table = held.tile([P, T], U8, name="e_scale_table", tag="e_scale_table", align_bytes=64)
+        inv_table = held.tile([P, T], F32, name="inv_table")
         half = held.tile([P, ATOM_BLOCKS], F32, name="half")
         warm = held.tile([P, 1], F32, name="warm")
         identity = held.tile([P, P], F32, name="identity")
         nc.gpsimd.memset(x_scale_table[:].bitcast(I32), 0)
         nc.vector.memset(inv_table[:, 0:1280].bitcast(I32), 0)
         nc.gpsimd.memset(inv_table[:, 1280:T].bitcast(I32), 0)
-        nc.vector.memset(half[:], 0.5)
         nc.gpsimd.memset(e_scale_table[:].bitcast(I32), 0)
+        nc.vector.memset(half[:], 0.5)
         make_identity(nc, identity[:])
         x_rows = x_scales[0].bitcast(I32).rearrange("(q r) c -> r q c", r=4)
         e_rows = e_scales[0].bitcast(I32).rearrange("(q r) c -> r q c", r=4)
-        nc.sync.dma_start(hr_raw[:], hr.rearrange("(p j) t -> p j t", j=PACK))
+        hr_rows = hr.rearrange("(p j) t -> p j t", j=PACK)
+        nc.sync.dma_start(raw[:, 0, 0:2, :], hr_rows[:, 0:2, :])
         for r in range(4):
-            nc.scalar.dma_start(x_scale_table[r:P:32, :].bitcast(I32), x_rows[r])
-        nc.scalar.dma_start(inv_table[0:1, :], inv[0:1, :])
+            nc.sync.dma_start(x_scale_table[r:P:32, :].bitcast(I32), x_rows[r])
+        nc.sync.dma_start(raw[:, 0, 2:4, :], hr_rows[:, 2:4, :])
+        nc.sync.dma_start(inv_table[0:1, :], inv[0:1, :])
         nc.scalar.activation(warm[:], half[:, 0:1], ACT.Exp)
-        nc.sync.dma_start(e_scale_table[E_PLANE:P:32, :].bitcast(I32), e_rows[0])
-        nc.sync.dma_start(hi_raw[:], hi.rearrange("(p j) t -> p j t", j=PACK))
-        nc.sync.dma_start(x_table[:], x_words[0].rearrange("p n r -> p (n r)").bitcast(I32))
-        for r in range(1, 4):
+        nc.sync.dma_start(raw[:, 1, :, :], hi.rearrange("(p j) t -> p j t", j=PACK))
+        for r in range(4):
             nc.sync.dma_start(e_scale_table[E_PLANE + r : P : 32, :].bitcast(I32), e_rows[r])
+        nc.sync.dma_start(x_table[:], x_words[0].rearrange("p n r -> p (n r)").bitcast(I32))
         nc.sync.dma_start(e_table[:], e_words[0].rearrange("p n r -> p (n r)").bitcast(I32))
 
         x_scale = held.tile([P, S], U8, name="x_scale", align_bytes=64)
@@ -80,36 +79,19 @@ def tile_picked_ymrf_steep_p_kernel(tc, x_words, x_scales, e_words, e_scales, hr
         turned = bank(7)
         for a in range(ATOM_BLOCKS):
             nc.tensor.transpose(turned[:, a * P : (a + 1) * P], inv_row[:, a * P : (a + 1) * P], identity[:])
-        inv_col = held.tile([P, ATOM_BLOCKS], F32, name="inv_col")
-        root = held.tile([P, ATOM_BLOCKS], F32, name="root")
-        nc.scalar.copy(inv_col[:], turned[:, 0:S:P])
-        nc.gpsimd.tensor_tensor(root[:], inv_col[:], half[:], ALU.pow)
 
-        codes = [held.tile([P, 3 * HALF], U32, name="codes%d" % h, align_bytes=64) for h in range(2)]
-        scales = [
-            reused.tile([P, 3 * HALF], U8, name="scales%d" % h, offset=4096 + 1024 * h, align_bytes=64) for h in range(2)
-        ]
-
-        def interleave(raw, h, name):
-            grouped = held.tile([P, PACK * HALF], BF16, name=name, align_bytes=64)
-            nc.scalar.copy(
-                grouped[:].rearrange("p (c i j) -> p c j i", i=4, j=PACK),
-                raw[:, :, h * HALF : (h + 1) * HALF].rearrange("p j (c i) -> p c j i", i=4),
+        def interleave(target, matrix, sign):
+            nc.scalar.activation(
+                target.rearrange("p (c i j) -> p c j i", i=4, j=PACK),
+                raw[:, matrix, :, 0:HALF].rearrange("p j (c i) -> p c j i", i=4),
+                ACT.Copy,
+                scale=sign,
             )
-            return grouped
 
-        def quantise(grouped, h, slot):
-            cols = slice(slot * HALF, (slot + 1) * HALF)
-            nc.vector.quantize_mx(out=codes[h][:, cols].bitcast(FP8X4), scales=scales[h][:, cols], in_=grouped[:])
-
-        for h in range(2):
-            plus = interleave(hr_raw, h, "hr_bf%d" % h)
-            minus = reused.tile([P, PACK * HALF], BF16, name="minus_hr_bf%d" % h, offset=2048 * h, align_bytes=64)
-            nc.vector.tensor_scalar(minus[:], plus[:], -1.0, None, ALU.mult)
-            quantise(plus, h, 0)
-            quantise(minus, h, 2)
-        for h in range(2):
-            quantise(interleave(hi_raw, h, "hi_bf%d" % h), h, 1)
+        def quantise(h, first_slot, slots):
+            cols = slice(first_slot * HALF, (first_slot + slots) * HALF)
+            values = grouped[h][:, PACK * cols.start : PACK * cols.stop]
+            nc.vector.quantize_mx(out=codes[h][:, cols].bitcast(FP8X4), scales=scales[h][:, cols], in_=values)
 
         def pick_words(table, name):
             picked = []
@@ -119,9 +101,39 @@ def tile_picked_ymrf_steep_p_kernel(tc, x_words, x_scales, e_words, e_scales, hr
                 picked.extend([words[:, 0:P], words[:, P : 2 * P]])
             return picked
 
-        x_picked = pick_words(x_table, "x_picked")
+        slot = PACK * HALF
         nc.vector.tensor_copy(e_scale[:], e_scale_table[:].indirect(offsets[:]))
+        codes = [
+            held.tile([P, 3 * HALF], U32, name="codes0", tag="e_scale_table", align_bytes=64),
+            held.tile([P, 3 * HALF], U32, name="codes1", align_bytes=64),
+        ]
+        grouped = [
+            held.tile([P, 3 * slot], BF16, name="grouped0", align_bytes=64),
+            held.tile([P, 2 * slot], BF16, name="grouped1", align_bytes=64),
+        ]
+        scales = [held.tile([P, 3 * HALF], U8, name="scales0", align_bytes=64)]
+        interleave(grouped[0][:, 0:slot], 0, 1.0)
+        interleave(grouped[0][:, 2 * slot : 3 * slot], 0, -1.0)
+        interleave(grouped[0][:, slot : 2 * slot], 1, 1.0)
+        quantise(0, 2, 1)
+        quantise(0, 0, 2)
+        x_picked = pick_words(x_table, "x_picked")
+        scales.append(held.tile([P, 3 * HALF], U8, name="scales1", tag="x_table", align_bytes=64))
+        nc.scalar.copy(
+            grouped[1][:].rearrange("p (m c i j) -> p m c j i", m=2, i=4, j=PACK),
+            raw[:, :, :, HALF:V].rearrange("p m j (c i) -> p m c j i", i=4),
+        )
+        quantise(1, 0, 2)
+        inv_col = held.tile([P, ATOM_BLOCKS], F32, name="inv_col", tag="raw")
+        root = held.tile([P, ATOM_BLOCKS], F32, name="root")
+        nc.scalar.copy(inv_col[:], turned[:, 0:S:P])
+        nc.gpsimd.tensor_tensor(root[:], inv_col[:], half[:], ALU.pow)
         e_picked = pick_words(e_table, "e_picked")
+        minus = held.tile([P, slot], BF16, name="minus", tag="e_table", align_bytes=64)
+        nc.vector.tensor_scalar(minus[:], grouped[1][:, 0:slot], -1.0, None, ALU.mult)
+        nc.vector.quantize_mx(
+            out=codes[1][:, 2 * HALF : 3 * HALF].bitcast(FP8X4), scales=scales[1][:, 2 * HALF : 3 * HALF], in_=minus[:]
+        )
 
         def product_pass(target, h, a, table, start):
             if table == "x":
@@ -138,9 +150,22 @@ def tile_picked_ymrf_steep_p_kernel(tc, x_words, x_scales, e_words, e_scales, hr
                 stop=not start,
             )
 
+        idle = bank(4)
+        for w in range(WARM_PASSES):
+            nc.tensor.matmul_mx(
+                out=idle[:, 0:HALF],
+                lhsT=codes[0][:, 2 * HALF : 2 * HALF + P].bitcast(FP8X4),
+                lhsT_scale=scales[0][:, 2 * HALF : 2 * HALF + P],
+                rhs=codes[0][:, 2 * HALF : 3 * HALF].bitcast(FP8X4),
+                rhs_scale=scales[0][:, 2 * HALF : 3 * HALF],
+                start=True,
+                stop=True,
+            )
+
         units = [(h, a) for h in range(2) for a in range(ATOM_BLOCKS)]
         products = {unit: bank(b) for b, unit in enumerate(units)}
         squares = {}
+        sums = {}
 
         def finish_unit(b):
             h, a = units[b]
@@ -149,49 +174,66 @@ def tile_picked_ymrf_steep_p_kernel(tc, x_words, x_scales, e_words, e_scales, hr
             if b >= EARLY_UNITS:
                 product_pass(target, h, a, "x", False)
             squares[h, a] = held.tile([P, 2 * HALF], F32, name="squares%d_%d" % (h, a))
-            if b == VECTOR_UNIT:
-                scaled = held.tile([P, 2 * HALF], F32, name="scaled")
-                parts = [slice(0, HALF), slice(HALF, 2 * HALF)]
-                for cols in parts:
-                    nc.vector.tensor_scalar(scaled[:, cols], target[:, cols], root[:, a : a + 1], None, ALU.mult)
-                for cols in parts:
-                    nc.vector.tensor_tensor(squares[h, a][:, cols], scaled[:, cols], scaled[:, cols], ALU.mult)
-            else:
-                nc.scalar.activation(squares[h, a][:], target[:], ACT.Square, scale=root[:, a : a + 1])
+            nc.scalar.activation(squares[h, a][:], target[:], ACT.Square, scale=root[:, a : a + 1])
+            if h == 0:
+                sums[a] = held.tile([P, HALF], F32, name="sums%d" % a)
+                nc.gpsimd.tensor_tensor(sums[a][:], squares[h, a][:, 0:HALF], squares[h, a][:, HALF : 2 * HALF], ALU.add)
 
-        def finish_block(v, match, pieces):
+        def turn(target, v, a):
             h, first = divmod(v * P, HALF)
-            for a in range(ATOM_BLOCKS):
-                for part in range(2):
-                    nc.tensor.matmul(
-                        match[:, a * P : (a + 1) * P],
-                        squares[h, a][:, part * HALF + first : part * HALF + first + P],
-                        identity[:],
-                        start=(part == 0),
-                        stop=(part == 1),
-                        is_transpose=True,
-                    )
-            sixth = held.tile([P, S], F32, name="sixth%d" % v)
-            top_sixth = held.tile([P, 1], F32, name="top_sixth%d" % v)
-            gain = held.tile([P, 1], F32, name="gain%d" % v)
+            if h == 0:
+                nc.tensor.transpose(target, sums[a][:, first : first + P], identity[:])
+                return
+            for part in range(2):
+                nc.tensor.matmul(
+                    target,
+                    squares[h, a][:, part * HALF + first : part * HALF + first + P],
+                    identity[:],
+                    start=(part == 0),
+                    stop=(part == 1),
+                    is_transpose=True,
+                )
+
+        sixth = [held.tile([P, S], F32, name="sixth%d" % v) for v in range(VOXEL_BLOCKS)]
+        gain = [held.tile([P, 1], F32, name="gain%d" % v) for v in range(VOXEL_BLOCKS)]
+        match = {}
+        top_sixth = {}
+
+        def match_piece(v, blocks, b):
+            cols = slice(blocks.start * P, blocks.stop * P)
+            piece = bank(b)[:, cols]
+            for a in blocks:
+                turn(piece[:, (a - blocks.start) * P : (a - blocks.start + 1) * P], v, a)
+            so_far = top_sixth.get(v)
+            top_sixth[v] = held.tile([P, 1], F32, name="top_sixth%d_%d" % (v, blocks.start))[:]
+            nc.vector.tensor_scalar(sixth[v][:, cols], piece, 1.0 / 6.0, so_far, ALU.mult, ALU.max, accum_out=top_sixth[v])
+            match.setdefault(v, []).append((cols, piece))
+            if blocks.stop == ATOM_BLOCKS:
+                nc.vector.reciprocal(gain[v][:], top_sixth[v])
+
+        def finish_block(v):
             weight = held.tile([P, S], F32, name="weight%d" % v)
             result = held.tile([P, S], F32, name="result%d" % v)
-            nc.vector.tensor_scalar(sixth[:], match[:], 1.0 / 6.0, None, ALU.mult, ALU.max, accum_out=top_sixth[:])
-            nc.vector.reciprocal(gain[:], top_sixth[:])
-            width = S // pieces
-            for first_col in range(0, S, width):
-                cols = slice(first_col, first_col + width)
-                nc.scalar.activation(weight[:, cols], match[:, cols], ACT.Exp, bias=math.log(6.0) - 6.0, scale=gain[:])
-                nc.vector.scalar_tensor_tensor(result[:, cols], sixth[:, cols], gain[:], weight[:, cols], ALU.mult, ALU.mult)
+            for cols, piece in match[v]:
+                nc.scalar.activation(weight[:, cols], piece, ACT.Exp, bias=math.log(6.0) - 6.0, scale=gain[v][:])
+                nc.vector.scalar_tensor_tensor(
+                    result[:, cols], sixth[v][:, cols], gain[v][:], weight[:, cols], ALU.mult, ALU.mult
+                )
                 nc.sync.dma_start(out[v * P : (v + 1) * P, cols], result[:, cols])
 
         for h, a in units[:EARLY_UNITS]:
             product_pass(products[h, a], h, a, "x", True)
-        for b in range(6):
+        for b in range(0, 6):
             finish_unit(b)
-        finish_block(0, bank(3), 1)
-        finish_block(1, bank(2), 1)
-        for b in range(6, 8):
-            finish_unit(b)
-        finish_block(2, bank(0), 1)
-        finish_block(3, bank(1), 2)
+        match_piece(0, range(0, 2), 0)
+        match_piece(1, range(0, 2), 1)
+        finish_unit(6)
+        match_piece(0, range(2, 4), 2)
+        match_piece(1, range(2, 4), 3)
+        finish_unit(7)
+        match_piece(2, range(0, 3), 4)
+        match_piece(3, range(0, 3), 5)
+        match_piece(2, range(3, 4), 6)
+        match_piece(3, range(3, 4), 7)
+        for v in range(VOXEL_BLOCKS):
+            finish_block(v)

@@ -25,13 +25,14 @@ ATOM_BLOCKS = S // P
 VOXEL_BLOCKS = V // P
 E_PLANE = 4
 EARLY_UNITS = 4
-WARM_PASSES = 6
+WARM_PASSES = 4
 
 
 def tile_picked_ymrf_steep_p_kernel(tc, x_words, x_scales, e_words, e_scales, hr, hi, inv, offs, out):
     nc = tc.nc
     with ExitStack() as ctx:
         held = ctx.enter_context(tc.tile_pool(name="held", bufs=1))
+        late = ctx.enter_context(tc.tile_pool(name="late", bufs=1))
         psum = ctx.enter_context(tc.psum_pool(name="psum", bufs=1))
 
         def bank(b):
@@ -41,11 +42,11 @@ def tile_picked_ymrf_steep_p_kernel(tc, x_words, x_scales, e_words, e_scales, hr
         nc.sync.dma_start(offsets[:], offs)
 
         raw = held.tile([P, 2, PACK, V], F32, name="raw", tag="raw")
-        x_table = held.tile([P, T], I32, name="x_table", tag="x_table", align_bytes=64)
-        e_table = held.tile([P, T], I32, name="e_table", tag="e_table", align_bytes=64)
+        x_table = held.tile([P, T], I32, name="x_table")
+        e_table = late.tile([P, T], I32, name="e_table", offset=0, align_bytes=64)
         x_scale_table = held.tile([P, T], U8, name="x_scale_table")
-        e_scale_table = held.tile([P, T], U8, name="e_scale_table", tag="e_scale_table", align_bytes=64)
-        inv_table = held.tile([P, T], F32, name="inv_table")
+        e_scale_table = held.tile([P, T], U8, name="e_scale_table")
+        inv_table = held.tile([P, T], F32, name="inv_table", tag="inv_table", align_bytes=64)
         half = held.tile([P, ATOM_BLOCKS], F32, name="half")
         warm = held.tile([P, 1], F32, name="warm")
         identity = held.tile([P, P], F32, name="identity")
@@ -104,7 +105,7 @@ def tile_picked_ymrf_steep_p_kernel(tc, x_words, x_scales, e_words, e_scales, hr
         slot = PACK * HALF
         nc.vector.tensor_copy(e_scale[:], e_scale_table[:].indirect(offsets[:]))
         codes = [
-            held.tile([P, 3 * HALF], U32, name="codes0", tag="e_scale_table", align_bytes=64),
+            held.tile([P, 3 * HALF], U32, name="codes0", tag="inv_table", align_bytes=64),
             held.tile([P, 3 * HALF], U32, name="codes1", align_bytes=64),
         ]
         grouped = [
@@ -115,22 +116,23 @@ def tile_picked_ymrf_steep_p_kernel(tc, x_words, x_scales, e_words, e_scales, hr
         interleave(grouped[0][:, 0:slot], 0, 1.0)
         interleave(grouped[0][:, 2 * slot : 3 * slot], 0, -1.0)
         interleave(grouped[0][:, slot : 2 * slot], 1, 1.0)
+        quantise(0, 0, 1)
         quantise(0, 2, 1)
-        quantise(0, 0, 2)
+        quantise(0, 1, 1)
         x_picked = pick_words(x_table, "x_picked")
-        scales.append(held.tile([P, 3 * HALF], U8, name="scales1", tag="x_table", align_bytes=64))
         nc.scalar.copy(
             grouped[1][:].rearrange("p (m c i j) -> p m c j i", m=2, i=4, j=PACK),
             raw[:, :, :, HALF:V].rearrange("p m j (c i) -> p m c j i", i=4),
         )
-        quantise(1, 0, 2)
         inv_col = held.tile([P, ATOM_BLOCKS], F32, name="inv_col", tag="raw")
         root = held.tile([P, ATOM_BLOCKS], F32, name="root")
         nc.scalar.copy(inv_col[:], turned[:, 0:S:P])
         nc.gpsimd.tensor_tensor(root[:], inv_col[:], half[:], ALU.pow)
         e_picked = pick_words(e_table, "e_picked")
-        minus = held.tile([P, slot], BF16, name="minus", tag="e_table", align_bytes=64)
+        minus = late.tile([P, slot], BF16, name="minus", offset=0, align_bytes=64)
+        scales.append(late.tile([P, 3 * HALF], U8, name="scales1", offset=2 * slot, align_bytes=64))
         nc.vector.tensor_scalar(minus[:], grouped[1][:, 0:slot], -1.0, None, ALU.mult)
+        quantise(1, 0, 2)
         nc.vector.quantize_mx(
             out=codes[1][:, 2 * HALF : 3 * HALF].bitcast(FP8X4), scales=scales[1][:, 2 * HALF : 3 * HALF], in_=minus[:]
         )
@@ -151,16 +153,17 @@ def tile_picked_ymrf_steep_p_kernel(tc, x_words, x_scales, e_words, e_scales, hr
             )
 
         idle = bank(4)
-        for w in range(WARM_PASSES):
-            nc.tensor.matmul_mx(
-                out=idle[:, 0:HALF],
-                lhsT=codes[0][:, 2 * HALF : 2 * HALF + P].bitcast(FP8X4),
-                lhsT_scale=scales[0][:, 2 * HALF : 2 * HALF + P],
-                rhs=codes[0][:, 2 * HALF : 3 * HALF].bitcast(FP8X4),
-                rhs_scale=scales[0][:, 2 * HALF : 3 * HALF],
-                start=True,
-                stop=True,
-            )
+        for first in (0, HALF):
+            for w in range(WARM_PASSES):
+                nc.tensor.matmul_mx(
+                    out=idle[:, 0:HALF],
+                    lhsT=codes[0][:, first : first + P].bitcast(FP8X4),
+                    lhsT_scale=scales[0][:, first : first + P],
+                    rhs=codes[0][:, first : first + HALF].bitcast(FP8X4),
+                    rhs_scale=scales[0][:, first : first + HALF],
+                    start=True,
+                    stop=True,
+                )
 
         units = [(h, a) for h in range(2) for a in range(ATOM_BLOCKS)]
         products = {unit: bank(b) for b, unit in enumerate(units)}
@@ -170,14 +173,15 @@ def tile_picked_ymrf_steep_p_kernel(tc, x_words, x_scales, e_words, e_scales, hr
         def finish_unit(b):
             h, a = units[b]
             target = products[h, a]
-            product_pass(target, h, a, "e", b >= EARLY_UNITS)
-            if b >= EARLY_UNITS:
-                product_pass(target, h, a, "x", False)
+            if h == 1:
+                product_pass(target, h, a, "x", True)
+            product_pass(target, h, a, "e", False)
             squares[h, a] = held.tile([P, 2 * HALF], F32, name="squares%d_%d" % (h, a))
             nc.scalar.activation(squares[h, a][:], target[:], ACT.Square, scale=root[:, a : a + 1])
             if h == 0:
                 sums[a] = held.tile([P, HALF], F32, name="sums%d" % a)
-                nc.gpsimd.tensor_tensor(sums[a][:], squares[h, a][:, 0:HALF], squares[h, a][:, HALF : 2 * HALF], ALU.add)
+                adder = nc.gpsimd if a < 2 else nc.vector
+                adder.tensor_tensor(sums[a][:], squares[h, a][:, 0:HALF], squares[h, a][:, HALF : 2 * HALF], ALU.add)
 
         def turn(target, v, a):
             h, first = divmod(v * P, HALF)

@@ -24,7 +24,7 @@ HALF = V // 2
 ATOM_BLOCKS = S // P
 VOXEL_BLOCKS = V // P
 E_PLANE = 4
-EARLY_UNITS = 4
+EARLY_UNITS = 6
 WARM_PASSES = 4
 
 
@@ -32,7 +32,6 @@ def tile_picked_ymrf_steep_p_kernel(tc, x_words, x_scales, e_words, e_scales, hr
     nc = tc.nc
     with ExitStack() as ctx:
         held = ctx.enter_context(tc.tile_pool(name="held", bufs=1))
-        late = ctx.enter_context(tc.tile_pool(name="late", bufs=1))
         psum = ctx.enter_context(tc.psum_pool(name="psum", bufs=1))
 
         def bank(b):
@@ -42,8 +41,8 @@ def tile_picked_ymrf_steep_p_kernel(tc, x_words, x_scales, e_words, e_scales, hr
         nc.sync.dma_start(offsets[:], offs)
 
         raw = held.tile([P, 2, PACK, V], F32, name="raw", tag="raw")
-        x_table = held.tile([P, T], I32, name="x_table")
-        e_table = late.tile([P, T], I32, name="e_table", offset=0, align_bytes=64)
+        x_table = held.tile([P, T], I32, name="x_table", tag="x_table", align_bytes=64)
+        e_table = held.tile([P, T], I32, name="e_table", tag="e_table", align_bytes=64)
         x_scale_table = held.tile([P, T], U8, name="x_scale_table")
         e_scale_table = held.tile([P, T], U8, name="e_scale_table")
         inv_table = held.tile([P, T], F32, name="inv_table", tag="inv_table", align_bytes=64)
@@ -65,9 +64,11 @@ def tile_picked_ymrf_steep_p_kernel(tc, x_words, x_scales, e_words, e_scales, hr
         nc.sync.dma_start(raw[:, 0, 2:4, :], hr_rows[:, 2:4, :])
         nc.sync.dma_start(inv_table[0:1, :], inv[0:1, :])
         nc.scalar.activation(warm[:], half[:, 0:1], ACT.Exp)
-        nc.sync.dma_start(raw[:, 1, :, :], hi.rearrange("(p j) t -> p j t", j=PACK))
+        hi_rows = hi.rearrange("(p j) t -> p j t", j=PACK)
+        nc.sync.dma_start(raw[:, 1, 0:2, :], hi_rows[:, 0:2, :])
         for r in range(4):
             nc.sync.dma_start(e_scale_table[E_PLANE + r : P : 32, :].bitcast(I32), e_rows[r])
+        nc.sync.dma_start(raw[:, 1, 2:4, :], hi_rows[:, 2:4, :])
         nc.sync.dma_start(x_table[:], x_words[0].rearrange("p n r -> p (n r)").bitcast(I32))
         nc.sync.dma_start(e_table[:], e_words[0].rearrange("p n r -> p (n r)").bitcast(I32))
 
@@ -124,15 +125,15 @@ def tile_picked_ymrf_steep_p_kernel(tc, x_words, x_scales, e_words, e_scales, hr
             grouped[1][:].rearrange("p (m c i j) -> p m c j i", m=2, i=4, j=PACK),
             raw[:, :, :, HALF:V].rearrange("p m j (c i) -> p m c j i", i=4),
         )
+        scales.append(held.tile([P, 3 * HALF], U8, name="scales1", tag="x_table", align_bytes=64))
+        quantise(1, 0, 2)
         inv_col = held.tile([P, ATOM_BLOCKS], F32, name="inv_col", tag="raw")
         root = held.tile([P, ATOM_BLOCKS], F32, name="root")
         nc.scalar.copy(inv_col[:], turned[:, 0:S:P])
         nc.gpsimd.tensor_tensor(root[:], inv_col[:], half[:], ALU.pow)
         e_picked = pick_words(e_table, "e_picked")
-        minus = late.tile([P, slot], BF16, name="minus", offset=0, align_bytes=64)
-        scales.append(late.tile([P, 3 * HALF], U8, name="scales1", offset=2 * slot, align_bytes=64))
+        minus = held.tile([P, slot], BF16, name="minus", tag="e_table", align_bytes=64)
         nc.vector.tensor_scalar(minus[:], grouped[1][:, 0:slot], -1.0, None, ALU.mult)
-        quantise(1, 0, 2)
         nc.vector.quantize_mx(
             out=codes[1][:, 2 * HALF : 3 * HALF].bitcast(FP8X4), scales=scales[1][:, 2 * HALF : 3 * HALF], in_=minus[:]
         )
@@ -173,10 +174,10 @@ def tile_picked_ymrf_steep_p_kernel(tc, x_words, x_scales, e_words, e_scales, hr
         def finish_unit(b):
             h, a = units[b]
             target = products[h, a]
-            if h == 1:
-                product_pass(target, h, a, "x", True)
-            product_pass(target, h, a, "e", False)
-            squares[h, a] = held.tile([P, 2 * HALF], F32, name="squares%d_%d" % (h, a))
+            product_pass(target, h, a, "e", b >= EARLY_UNITS)
+            if b >= EARLY_UNITS:
+                product_pass(target, h, a, "x", False)
+            squares[h, a] = held.tile([P, 2 * HALF], F32, name="squares%d_%d" % (h, a), tag="squares%d_%d" % (h, a))
             nc.scalar.activation(squares[h, a][:], target[:], ACT.Square, scale=root[:, a : a + 1])
             if h == 0:
                 sums[a] = held.tile([P, HALF], F32, name="sums%d" % a)
@@ -209,7 +210,7 @@ def tile_picked_ymrf_steep_p_kernel(tc, x_words, x_scales, e_words, e_scales, hr
             for a in blocks:
                 turn(piece[:, (a - blocks.start) * P : (a - blocks.start + 1) * P], v, a)
             so_far = top_sixth.get(v)
-            top_sixth[v] = held.tile([P, 1], F32, name="top_sixth%d_%d" % (v, blocks.start))[:]
+            top_sixth[v] = held.tile([P, 1], F32, name="top%d_%d" % (v, blocks.start), tag="top%d_%d" % (v, blocks.start))[:]
             nc.vector.tensor_scalar(sixth[v][:, cols], piece, 1.0 / 6.0, so_far, ALU.mult, ALU.max, accum_out=top_sixth[v])
             match.setdefault(v, []).append((cols, piece))
             if blocks.stop == ATOM_BLOCKS:
@@ -217,7 +218,7 @@ def tile_picked_ymrf_steep_p_kernel(tc, x_words, x_scales, e_words, e_scales, hr
 
         def finish_block(v):
             weight = held.tile([P, S], F32, name="weight%d" % v)
-            result = held.tile([P, S], F32, name="result%d" % v)
+            result = held.tile([P, S], F32, name="result%d" % v, tag=["squares1_2", "top3_3", "result2", "result3"][v])
             for cols, piece in match[v]:
                 nc.scalar.activation(weight[:, cols], piece, ACT.Exp, bias=math.log(6.0) - 6.0, scale=gain[v][:])
                 nc.vector.scalar_tensor_tensor(

@@ -25,7 +25,6 @@ ATOM_BLOCKS = S // P
 VOXEL_BLOCKS = V // P
 E_PLANE = 4
 EARLY_UNITS = 6
-WARM_PASSES = 4
 
 
 def tile_picked_ymrf_steep_p_kernel(tc, x_words, x_scales, e_words, e_scales, hr, hi, inv, offs, out):
@@ -47,7 +46,6 @@ def tile_picked_ymrf_steep_p_kernel(tc, x_words, x_scales, e_words, e_scales, hr
         e_scale_table = held.tile([P, T], U8, name="e_scale_table")
         inv_table = held.tile([P, T], F32, name="inv_table", tag="inv_table", align_bytes=64)
         half = held.tile([P, ATOM_BLOCKS], F32, name="half")
-        warm = held.tile([P, 1], F32, name="warm")
         identity = held.tile([P, P], F32, name="identity")
         nc.gpsimd.memset(x_scale_table[:].bitcast(I32), 0)
         nc.vector.memset(inv_table[:, 0:1280].bitcast(I32), 0)
@@ -63,7 +61,6 @@ def tile_picked_ymrf_steep_p_kernel(tc, x_words, x_scales, e_words, e_scales, hr
             nc.sync.dma_start(x_scale_table[r:P:32, :].bitcast(I32), x_rows[r])
         nc.sync.dma_start(raw[:, 0, 2:4, :], hr_rows[:, 2:4, :])
         nc.sync.dma_start(inv_table[0:1, :], inv[0:1, :])
-        nc.scalar.activation(warm[:], half[:, 0:1], ACT.Exp)
         hi_rows = hi.rearrange("(p j) t -> p j t", j=PACK)
         nc.sync.dma_start(raw[:, 1, 0:2, :], hi_rows[:, 0:2, :])
         for r in range(4):
@@ -152,19 +149,6 @@ def tile_picked_ymrf_steep_p_kernel(tc, x_words, x_scales, e_words, e_scales, hr
                 start=start,
                 stop=not start,
             )
-
-        idle = bank(4)
-        for first in (0, HALF):
-            for w in range(WARM_PASSES):
-                nc.tensor.matmul_mx(
-                    out=idle[:, 0:HALF],
-                    lhsT=codes[0][:, first : first + P].bitcast(FP8X4),
-                    lhsT_scale=scales[0][:, first : first + P],
-                    rhs=codes[0][:, first : first + HALF].bitcast(FP8X4),
-                    rhs_scale=scales[0][:, first : first + HALF],
-                    start=True,
-                    stop=True,
-                )
 
         units = [(h, a) for h in range(2) for a in range(ATOM_BLOCKS)]
         products = {unit: bank(b) for b, unit in enumerate(units)}

@@ -20,11 +20,8 @@ ACT = mybir.ActivationFunctionType
 
 P = 128
 PACK = 4
-HALF = V // 2
-ATOM_BLOCKS = S // P
-VOXEL_BLOCKS = V // P
+BLOCKS = 4
 E_PLANE = 4
-EARLY_UNITS = 6
 
 
 def tile_picked_ymrf_steep_p_kernel(tc, x_words, x_scales, e_words, e_scales, hr, hi, inv, offs, out):
@@ -37,60 +34,49 @@ def tile_picked_ymrf_steep_p_kernel(tc, x_words, x_scales, e_words, e_scales, hr
             return psum.tile([P, 512], F32, name="bank%d" % b, tag="bank%d" % b)
 
         offsets = held.tile([P, S // 16], U16, name="offsets")
-        nc.sync.dma_start(offsets[:], offs)
-
-        raw = held.tile([P, 2, PACK, V], F32, name="raw", tag="raw")
-        x_table = held.tile([P, T], I32, name="x_table", tag="x_table", align_bytes=64)
-        e_table = held.tile([P, T], I32, name="e_table", tag="e_table", align_bytes=64)
+        x_table = held.tile([P, T], I32, name="x_table", align_bytes=64)
+        e_table = held.tile([P, T], I32, name="e_table", align_bytes=64)
         x_scale_table = held.tile([P, T], U8, name="x_scale_table")
         e_scale_table = held.tile([P, T], U8, name="e_scale_table")
         inv_table = held.tile([P, T], F32, name="inv_table", tag="inv_table", align_bytes=64)
-        half = held.tile([P, ATOM_BLOCKS], F32, name="half")
+        half = held.tile([P, BLOCKS], F32, name="half")
+        warm = held.tile([P, 1], F32, name="warm")
         identity = held.tile([P, P], F32, name="identity")
+        raw = [[held.tile([P, PACK, P], F32, name="raw%d_%d" % (v, m)) for m in range(2)] for v in range(BLOCKS)]
+        signal_rows = [m.rearrange("(p j) t -> p j t", j=PACK) for m in (hr, hi)]
+
+        def load_signal(v, m):
+            nc.sync.dma_start(raw[v][m][:], signal_rows[m][:, :, v * P : (v + 1) * P])
+
         nc.gpsimd.memset(x_scale_table[:].bitcast(I32), 0)
-        nc.vector.memset(inv_table[:, 0:1280].bitcast(I32), 0)
-        nc.gpsimd.memset(inv_table[:, 1280:T].bitcast(I32), 0)
-        nc.gpsimd.memset(e_scale_table[:].bitcast(I32), 0)
+        nc.vector.memset(inv_table[:, 0:511].bitcast(I32), 0)
+        nc.vector.memset(inv_table[:, 511:1024].bitcast(I32), 0)
+        nc.gpsimd.memset(inv_table[:, 1024:T].bitcast(I32), 0)
         nc.vector.memset(half[:], 0.5)
+        nc.gpsimd.memset(e_scale_table[:].bitcast(I32), 0)
         make_identity(nc, identity[:])
+
         x_rows = x_scales[0].bitcast(I32).rearrange("(q r) c -> r q c", r=4)
         e_rows = e_scales[0].bitcast(I32).rearrange("(q r) c -> r q c", r=4)
-        hr_rows = hr.rearrange("(p j) t -> p j t", j=PACK)
-        nc.sync.dma_start(raw[:, 0, 0:2, :], hr_rows[:, 0:2, :])
+        load_signal(0, 0)
+        nc.sync.dma_start(offsets[:], offs)
         for r in range(4):
             nc.sync.dma_start(x_scale_table[r:P:32, :].bitcast(I32), x_rows[r])
-        nc.sync.dma_start(raw[:, 0, 2:4, :], hr_rows[:, 2:4, :])
-        nc.sync.dma_start(inv_table[0:1, :], inv[0:1, :])
-        hi_rows = hi.rearrange("(p j) t -> p j t", j=PACK)
-        nc.sync.dma_start(raw[:, 1, 0:2, :], hi_rows[:, 0:2, :])
+        nc.sync.dma_start(x_table[:], x_words[0].rearrange("p n r -> p (n r)").bitcast(I32))
         for r in range(4):
             nc.sync.dma_start(e_scale_table[E_PLANE + r : P : 32, :].bitcast(I32), e_rows[r])
-        nc.sync.dma_start(raw[:, 1, 2:4, :], hi_rows[:, 2:4, :])
-        nc.sync.dma_start(x_table[:], x_words[0].rearrange("p n r -> p (n r)").bitcast(I32))
+        load_signal(0, 1)
         nc.sync.dma_start(e_table[:], e_words[0].rearrange("p n r -> p (n r)").bitcast(I32))
+        for v in range(1, BLOCKS):
+            load_signal(v, 0)
+            load_signal(v, 1)
+        nc.scalar.dma_start(inv_table[0:1, :], inv[0:1, :])
+        nc.scalar.activation(warm[:], half[:, 0:1], ACT.Exp)
 
         x_scale = held.tile([P, S], U8, name="x_scale", align_bytes=64)
-        e_scale = held.tile([P, S], U8, name="e_scale", align_bytes=64)
         inv_row = held.tile([P, S], F32, name="inv_row")
         nc.vector.tensor_copy(x_scale[:], x_scale_table[:].indirect(offsets[:]))
         nc.vector.tensor_copy(inv_row[:], inv_table[:].indirect(offsets[:]))
-
-        turned = bank(7)
-        for a in range(ATOM_BLOCKS):
-            nc.tensor.transpose(turned[:, a * P : (a + 1) * P], inv_row[:, a * P : (a + 1) * P], identity[:])
-
-        def interleave(target, matrix, sign):
-            nc.scalar.activation(
-                target.rearrange("p (c i j) -> p c j i", i=4, j=PACK),
-                raw[:, matrix, :, 0:HALF].rearrange("p j (c i) -> p c j i", i=4),
-                ACT.Copy,
-                scale=sign,
-            )
-
-        def quantise(h, first_slot, slots):
-            cols = slice(first_slot * HALF, (first_slot + slots) * HALF)
-            values = grouped[h][:, PACK * cols.start : PACK * cols.stop]
-            nc.vector.quantize_mx(out=codes[h][:, cols].bitcast(FP8X4), scales=scales[h][:, cols], in_=values)
 
         def pick_words(table, name):
             picked = []
@@ -100,129 +86,137 @@ def tile_picked_ymrf_steep_p_kernel(tc, x_words, x_scales, e_words, e_scales, hr
                 picked.extend([words[:, 0:P], words[:, P : 2 * P]])
             return picked
 
-        slot = PACK * HALF
-        nc.vector.tensor_copy(e_scale[:], e_scale_table[:].indirect(offsets[:]))
-        codes = [
-            held.tile([P, 3 * HALF], U32, name="codes0", tag="inv_table", align_bytes=64),
-            held.tile([P, 3 * HALF], U32, name="codes1", align_bytes=64),
-        ]
-        grouped = [
-            held.tile([P, 3 * slot], BF16, name="grouped0", align_bytes=64),
-            held.tile([P, 2 * slot], BF16, name="grouped1", align_bytes=64),
-        ]
-        scales = [held.tile([P, 3 * HALF], U8, name="scales0", align_bytes=64)]
-        interleave(grouped[0][:, 0:slot], 0, 1.0)
-        interleave(grouped[0][:, 2 * slot : 3 * slot], 0, -1.0)
-        interleave(grouped[0][:, slot : 2 * slot], 1, 1.0)
-        quantise(0, 0, 1)
-        quantise(0, 2, 1)
-        quantise(0, 1, 1)
         x_picked = pick_words(x_table, "x_picked")
-        nc.scalar.copy(
-            grouped[1][:].rearrange("p (m c i j) -> p m c j i", m=2, i=4, j=PACK),
-            raw[:, :, :, HALF:V].rearrange("p m j (c i) -> p m c j i", i=4),
-        )
-        scales.append(held.tile([P, 3 * HALF], U8, name="scales1", tag="x_table", align_bytes=64))
-        quantise(1, 0, 2)
-        inv_col = held.tile([P, ATOM_BLOCKS], F32, name="inv_col", tag="raw")
-        root = held.tile([P, ATOM_BLOCKS], F32, name="root")
-        nc.scalar.copy(inv_col[:], turned[:, 0:S:P])
-        nc.gpsimd.tensor_tensor(root[:], inv_col[:], half[:], ALU.pow)
-        e_picked = pick_words(e_table, "e_picked")
-        minus = held.tile([P, slot], BF16, name="minus", tag="e_table", align_bytes=64)
-        nc.vector.tensor_scalar(minus[:], grouped[1][:, 0:slot], -1.0, None, ALU.mult)
-        nc.vector.quantize_mx(
-            out=codes[1][:, 2 * HALF : 3 * HALF].bitcast(FP8X4), scales=scales[1][:, 2 * HALF : 3 * HALF], in_=minus[:]
-        )
+        e_scale = held.tile([P, S], U8, name="e_scale", tag="inv_table", align_bytes=64)
+        nc.vector.tensor_copy(e_scale[:], e_scale_table[:].indirect(offsets[:]))
 
-        def product_pass(target, h, a, table, start):
+        turned = bank(7)
+        for a in range(BLOCKS):
+            nc.tensor.transpose(turned[:, a * P : (a + 1) * P], inv_row[:, a * P : (a + 1) * P], identity[:])
+
+        codes = [held.tile([P, 3 * P], U32, name="codes%d" % v, align_bytes=64) for v in range(BLOCKS)]
+        scales = [held.tile([P, 3 * P], U8, name="scales%d" % v, align_bytes=64) for v in range(BLOCKS)]
+        grouped = [[held.tile([P, PACK * P], BF16, name="grouped%d_%d" % (v, s), align_bytes=64) for s in range(3)] for v in range(BLOCKS)]
+
+        def views(v, slot, m):
+            return (
+                grouped[v][slot][:].rearrange("p (c i j) -> p c j i", i=4, j=PACK),
+                raw[v][m][:].rearrange("p j (c i) -> p c j i", i=4),
+            )
+
+        def cast_scalar(v, slot, m, sign):
+            target, source = views(v, slot, m)
+            nc.scalar.activation(target, source, ACT.Copy, scale=sign)
+
+        def cast_vector(v, slot, m):
+            target, source = views(v, slot, m)
+            nc.vector.tensor_copy(target, source)
+
+        def negate_vector(v):
+            nc.vector.tensor_scalar(grouped[v][2][:], grouped[v][0][:], -1.0, None, ALU.mult)
+
+        def quantise(v, slot):
+            cols = slice(slot * P, (slot + 1) * P)
+            nc.vector.quantize_mx(out=codes[v][:, cols].bitcast(FP8X4), scales=scales[v][:, cols], in_=grouped[v][slot][:])
+
+        def product_pass(target, v, a, table, start, stop):
             if table == "x":
                 words, plane, first = x_picked[a], x_scale[:, a * P : (a + 1) * P], 0
             else:
-                words, plane, first = e_picked[a], e_scale[E_PLANE:P, a * P : (a + 1) * P], HALF
+                words, plane, first = e_picked[a], e_scale[E_PLANE:P, a * P : (a + 1) * P], P
             nc.tensor.matmul_mx(
-                out=target[:],
+                out=target,
                 lhsT=words.bitcast(FP8X4),
                 lhsT_scale=plane,
-                rhs=codes[h][:, first : first + 2 * HALF].bitcast(FP8X4),
-                rhs_scale=scales[h][:, first : first + 2 * HALF],
+                rhs=codes[v][:, first : first + 2 * P].bitcast(FP8X4),
+                rhs_scale=scales[v][:, first : first + 2 * P],
                 start=start,
-                stop=not start,
+                stop=stop,
             )
 
-        units = [(h, a) for h in range(2) for a in range(ATOM_BLOCKS)]
-        products = {unit: bank(b) for b, unit in enumerate(units)}
+        products = {}
         squares = {}
-        sums = {}
 
-        def finish_unit(b):
-            h, a = units[b]
-            target = products[h, a]
-            product_pass(target, h, a, "e", b >= EARLY_UNITS)
-            if b >= EARLY_UNITS:
-                product_pass(target, h, a, "x", False)
-            squares[h, a] = held.tile([P, 2 * HALF], F32, name="squares%d_%d" % (h, a), tag="squares%d_%d" % (h, a))
-            nc.scalar.activation(squares[h, a][:], target[:], ACT.Square, scale=root[:, a : a + 1])
-            if h == 0:
-                sums[a] = held.tile([P, HALF], F32, name="sums%d" % a)
-                adder = nc.gpsimd if a < 2 else nc.vector
-                adder.tensor_tensor(sums[a][:], squares[h, a][:, 0:HALF], squares[h, a][:, HALF : 2 * HALF], ALU.add)
+        def open_products(v):
+            for u in range(2):
+                tile = bank(2 * (v % 2) + u)
+                for a in (2 * u, 2 * u + 1):
+                    products[v, a] = tile[:, (a % 2) * 2 * P : (a % 2 + 1) * 2 * P]
 
-        def turn(target, v, a):
-            h, first = divmod(v * P, HALF)
-            if h == 0:
-                nc.tensor.transpose(target, sums[a][:, first : first + P], identity[:])
-                return
-            for part in range(2):
-                nc.tensor.matmul(
-                    target,
-                    squares[h, a][:, part * HALF + first : part * HALF + first + P],
-                    identity[:],
-                    start=(part == 0),
-                    stop=(part == 1),
-                    is_transpose=True,
-                )
+        def multiply(v):
+            open_products(v)
+            for a in range(BLOCKS):
+                product_pass(products[v, a], v, a, "x", True, False)
+                product_pass(products[v, a], v, a, "e", False, True)
 
-        sixth = [held.tile([P, S], F32, name="sixth%d" % v) for v in range(VOXEL_BLOCKS)]
-        gain = [held.tile([P, 1], F32, name="gain%d" % v) for v in range(VOXEL_BLOCKS)]
+        def square(v):
+            for a in range(BLOCKS):
+                squares[v, a] = held.tile([P, 2 * P], F32, name="squares%d_%d" % (v, a))
+                nc.scalar.activation(squares[v, a][:], products[v, a], ACT.Square, scale=root[:, a : a + 1])
+
         match = {}
-        top_sixth = {}
+        sixth = [held.tile([P, S], F32, name="sixth%d" % v) for v in range(BLOCKS)]
+        top_sixth = [held.tile([P, 1], F32, name="top%d" % v) for v in range(BLOCKS)]
+        gain = [held.tile([P, 1], F32, name="gain%d" % v) for v in range(BLOCKS)]
+        weight = [held.tile([P, S], F32, name="weight%d" % v) for v in range(BLOCKS)]
+        result = [held.tile([P, S], F32, name="result%d" % v) for v in range(BLOCKS)]
 
-        def match_piece(v, blocks, b):
-            cols = slice(blocks.start * P, blocks.stop * P)
-            piece = bank(b)[:, cols]
-            for a in blocks:
-                turn(piece[:, (a - blocks.start) * P : (a - blocks.start + 1) * P], v, a)
-            so_far = top_sixth.get(v)
-            top_sixth[v] = held.tile([P, 1], F32, name="top%d_%d" % (v, blocks.start), tag="top%d_%d" % (v, blocks.start))[:]
-            nc.vector.tensor_scalar(sixth[v][:, cols], piece, 1.0 / 6.0, so_far, ALU.mult, ALU.max, accum_out=top_sixth[v])
-            match.setdefault(v, []).append((cols, piece))
-            if blocks.stop == ATOM_BLOCKS:
-                nc.vector.reciprocal(gain[v][:], top_sixth[v])
+        def turn(v):
+            match[v] = bank(4 + v)
+            for a in range(BLOCKS):
+                for part in range(2):
+                    nc.tensor.matmul(
+                        match[v][:, a * P : (a + 1) * P],
+                        squares[v, a][:, part * P : (part + 1) * P],
+                        identity[:],
+                        start=(part == 0),
+                        stop=(part == 1),
+                        is_transpose=True,
+                    )
 
-        def finish_block(v):
-            weight = held.tile([P, S], F32, name="weight%d" % v)
-            result = held.tile([P, S], F32, name="result%d" % v, tag=["squares1_2", "top3_3", "result2", "result3"][v])
-            for cols, piece in match[v]:
-                nc.scalar.activation(weight[:, cols], piece, ACT.Exp, bias=math.log(6.0) - 6.0, scale=gain[v][:])
-                nc.vector.scalar_tensor_tensor(
-                    result[:, cols], sixth[v][:, cols], gain[v][:], weight[:, cols], ALU.mult, ALU.mult
-                )
-                nc.sync.dma_start(out[v * P : (v + 1) * P, cols], result[:, cols])
+        def best(v):
+            nc.vector.tensor_scalar(sixth[v][:], match[v][:], 1.0 / 6.0, None, ALU.mult, ALU.max, accum_out=top_sixth[v][:])
+            nc.vector.reciprocal(gain[v][:], top_sixth[v][:])
 
-        for h, a in units[:EARLY_UNITS]:
-            product_pass(products[h, a], h, a, "x", True)
-        for b in range(0, 6):
-            finish_unit(b)
-        match_piece(0, range(0, 2), 0)
-        match_piece(1, range(0, 2), 1)
-        finish_unit(6)
-        match_piece(0, range(2, 4), 2)
-        match_piece(1, range(2, 4), 3)
-        finish_unit(7)
-        match_piece(2, range(0, 3), 4)
-        match_piece(3, range(0, 3), 5)
-        match_piece(2, range(3, 4), 6)
-        match_piece(3, range(3, 4), 7)
-        for v in range(VOXEL_BLOCKS):
-            finish_block(v)
+        def finish(v, pieces):
+            width = S // pieces
+            for u in range(pieces):
+                cols = slice(u * width, (u + 1) * width)
+                nc.scalar.activation(weight[v][:, cols], match[v][:, cols], ACT.Exp, bias=math.log(6.0) - 6.0, scale=gain[v][:])
+                nc.vector.scalar_tensor_tensor(result[v][:, cols], sixth[v][:, cols], gain[v][:], weight[v][:, cols], ALU.mult, ALU.mult)
+                nc.sync.dma_start(out[v * P : (v + 1) * P, cols], result[v][:, cols])
+
+        cast_scalar(0, 0, 0, 1.0)
+        cast_scalar(0, 2, 0, -1.0)
+        cast_scalar(0, 1, 1, 1.0)
+        for slot in (0, 2, 1):
+            quantise(0, slot)
+        inv_col = held.tile([P, BLOCKS], F32, name="inv_col")
+        root = held.tile([P, BLOCKS], F32, name="root")
+        nc.scalar.copy(inv_col[:], turned[:, 0:S:P])
+        nc.gpsimd.tensor_tensor(root[:], inv_col[:], half[:], ALU.pow)
+
+        open_products(0)
+        for a in range(BLOCKS):
+            product_pass(products[0, a], 0, a, "x", a % 2 == 0, False)
+        e_picked = pick_words(e_table, "e_picked")
+        for a in range(BLOCKS):
+            product_pass(products[0, a], 0, a, "e", False, a % 2 == 1)
+        cast_scalar(1, 0, 0, 1.0)
+        square(0)
+        for v in range(1, BLOCKS):
+            if v > 1:
+                cast_vector(v, 0, 0)
+            negate_vector(v)
+            quantise(v, 0)
+            quantise(v, 2)
+            cast_vector(v, 1, 1)
+            quantise(v, 1)
+            multiply(v)
+            turn(v - 1)
+            square(v)
+        turn(BLOCKS - 1)
+        for v in range(BLOCKS):
+            best(v)
+        for v in range(BLOCKS):
+            finish(v, 2 if v == BLOCKS - 1 else 1)

@@ -22,6 +22,8 @@ P = 128
 PACK = 4
 BLOCKS = 4
 E_PLANE = 4
+HALF = V // 2
+POOL_BLOCKS = 1
 
 
 def tile_picked_ymrf_steep_p_kernel(tc, x_words, x_scales, e_words, e_scales, hr, hi, inv, offs, out):
@@ -34,24 +36,25 @@ def tile_picked_ymrf_steep_p_kernel(tc, x_words, x_scales, e_words, e_scales, hr
             return psum.tile([P, 512], F32, name="bank%d" % b, tag="bank%d" % b)
 
         offsets = held.tile([P, S // 16], U16, name="offsets")
-        x_table = held.tile([P, T], I32, name="x_table", align_bytes=64)
-        e_table = held.tile([P, T], I32, name="e_table", align_bytes=64)
+        x_table = held.tile([P, T], I32, name="x_table", tag="x_table", align_bytes=64)
+        e_table = held.tile([P, T], I32, name="e_table", tag="e_table", align_bytes=64)
         x_scale_table = held.tile([P, T], U8, name="x_scale_table")
-        e_scale_table = held.tile([P, T], U8, name="e_scale_table")
+        e_scale_table = held.tile([P, T], U8, name="e_scale_table", tag="e_scale_table", align_bytes=64)
         inv_table = held.tile([P, T], F32, name="inv_table", tag="inv_table", align_bytes=64)
         half = held.tile([P, BLOCKS], F32, name="half")
         warm = held.tile([P, 1], F32, name="warm")
         identity = held.tile([P, P], F32, name="identity")
-        raw = [[held.tile([P, PACK, P], F32, name="raw%d_%d" % (v, m)) for m in range(2)] for v in range(BLOCKS)]
+        raw = {(m, g): held.tile([P, PACK, HALF], F32, name="raw%d_%d" % (m, g), tag="raw%d_%d" % (m, g)) for m, g in ((0, 0), (0, 1), (1, 0))}
+        raw_last = [held.tile([P, PACK, P], F32, name="raw_last%d" % u) for u in range(2)]
         signal_rows = [m.rearrange("(p j) t -> p j t", j=PACK) for m in (hr, hi)]
 
-        def load_signal(v, m):
-            nc.sync.dma_start(raw[v][m][:], signal_rows[m][:, :, v * P : (v + 1) * P])
+        def load_signal(m, g):
+            nc.sync.dma_start(raw[m, g][:], signal_rows[m][:, :, g * HALF : (g + 1) * HALF])
 
         nc.gpsimd.memset(x_scale_table[:].bitcast(I32), 0)
-        nc.vector.memset(inv_table[:, 0:511].bitcast(I32), 0)
-        nc.vector.memset(inv_table[:, 511:1024].bitcast(I32), 0)
-        nc.gpsimd.memset(inv_table[:, 1024:T].bitcast(I32), 0)
+        nc.vector.memset(inv_table[:, 0:575].bitcast(I32), 0)
+        nc.vector.memset(inv_table[:, 575:1152].bitcast(I32), 0)
+        nc.gpsimd.memset(inv_table[:, 1152:T].bitcast(I32), 0)
         nc.vector.memset(half[:], 0.5)
         nc.gpsimd.memset(e_scale_table[:].bitcast(I32), 0)
         make_identity(nc, identity[:])
@@ -62,161 +65,200 @@ def tile_picked_ymrf_steep_p_kernel(tc, x_words, x_scales, e_words, e_scales, hr
         nc.sync.dma_start(offsets[:], offs)
         for r in range(4):
             nc.sync.dma_start(x_scale_table[r:P:32, :].bitcast(I32), x_rows[r])
+        nc.sync.dma_start(inv_table[0:1, :], inv[0:1, :])
         nc.sync.dma_start(x_table[:], x_words[0].rearrange("p n r -> p (n r)").bitcast(I32))
         for r in range(4):
             nc.sync.dma_start(e_scale_table[E_PLANE + r : P : 32, :].bitcast(I32), e_rows[r])
         load_signal(0, 1)
+        load_signal(1, 0)
         nc.sync.dma_start(e_table[:], e_words[0].rearrange("p n r -> p (n r)").bitcast(I32))
-        for v in range(1, BLOCKS):
-            load_signal(v, 0)
-            load_signal(v, 1)
-        nc.scalar.dma_start(inv_table[0:1, :], inv[0:1, :])
+        for u in range(2):
+            nc.sync.dma_start(raw_last[u][:], signal_rows[1][:, :, HALF + u * P : HALF + (u + 1) * P])
         nc.scalar.activation(warm[:], half[:, 0:1], ACT.Exp)
 
         x_scale = held.tile([P, S], U8, name="x_scale", align_bytes=64)
+        e_scale = held.tile([P, S], U8, name="e_scale", align_bytes=64)
         inv_row = held.tile([P, S], F32, name="inv_row")
         nc.vector.tensor_copy(x_scale[:], x_scale_table[:].indirect(offsets[:]))
         nc.vector.tensor_copy(inv_row[:], inv_table[:].indirect(offsets[:]))
 
-        def pick_words(table, name):
+        def pick_words(table, name, pieces):
             picked = []
-            for u in range(2):
-                words = held.tile([P, S // 2], U32, name="%s%d" % (name, u), align_bytes=64)
-                nc.vector.tensor_copy(words[:], table[:].bitcast(U32).indirect(offsets[:, u * 16 : (u + 1) * 16]))
-                picked.extend([words[:, 0:P], words[:, P : 2 * P]])
+            count = S // pieces
+            for u in range(pieces):
+                words = held.tile([P, count], U32, name="%s%d" % (name, u), align_bytes=64)
+                nc.vector.tensor_copy(words[:], table[:].bitcast(U32).indirect(offsets[:, u * count // 16 : (u + 1) * count // 16]))
+                picked.extend([words[:, c : c + P] for c in range(0, count, P)])
             return picked
-
-        x_picked = pick_words(x_table, "x_picked")
-        e_scale = held.tile([P, S], U8, name="e_scale", tag="inv_table", align_bytes=64)
-        nc.vector.tensor_copy(e_scale[:], e_scale_table[:].indirect(offsets[:]))
 
         turned = bank(7)
         for a in range(BLOCKS):
             nc.tensor.transpose(turned[:, a * P : (a + 1) * P], inv_row[:, a * P : (a + 1) * P], identity[:])
 
-        codes = [held.tile([P, 3 * P], U32, name="codes%d" % v, align_bytes=64) for v in range(BLOCKS)]
-        scales = [held.tile([P, 3 * P], U8, name="scales%d" % v, align_bytes=64) for v in range(BLOCKS)]
-        grouped = [[held.tile([P, PACK * P], BF16, name="grouped%d_%d" % (v, s), align_bytes=64) for s in range(3)] for v in range(BLOCKS)]
+        slot = PACK * HALF
+        codes = [held.tile([P, 3 * HALF], U32, name="codes%d" % g, align_bytes=64) for g in range(2)]
+        scales = [held.tile([P, 3 * HALF], U8, name="scales%d" % g, tag=("inv_table", "e_scale_table")[g], align_bytes=64) for g in range(2)]
+        grouped = {(g, s): held.tile([P, slot], BF16, name="grouped%d_%d" % (g, s), align_bytes=64) for g in range(2) for s in range(3) if (g, s) != (1, 1)}
+        last = [held.tile([P, slot // 2], BF16, name="last%d" % u, tag="last%d" % u, align_bytes=64) for u in range(2)]
 
-        def views(v, slot, m):
+        def views(g, s):
             return (
-                grouped[v][slot][:].rearrange("p (c i j) -> p c j i", i=4, j=PACK),
-                raw[v][m][:].rearrange("p j (c i) -> p c j i", i=4),
+                grouped[g, s][:].rearrange("p (c i j) -> p c j i", i=4, j=PACK),
+                raw[s % 2, g][:].rearrange("p j (c i) -> p c j i", i=4),
             )
 
-        def cast_scalar(v, slot, m, sign):
-            target, source = views(v, slot, m)
-            nc.scalar.activation(target, source, ACT.Copy, scale=sign)
+        def cast_scalar(g, s):
+            target, source = views(g, s)
+            nc.scalar.activation(target, source, ACT.Copy, scale=-1.0 if s == 2 else 1.0)
 
-        def cast_vector(v, slot, m):
-            target, source = views(v, slot, m)
-            nc.vector.tensor_copy(target, source)
+        def quantise(g, first, values):
+            cols = slice(first, first + values.shape[1] // PACK)
+            nc.vector.quantize_mx(out=codes[g][:, cols].bitcast(FP8X4), scales=scales[g][:, cols], in_=values)
 
-        def negate_vector(v):
-            nc.vector.tensor_scalar(grouped[v][2][:], grouped[v][0][:], -1.0, None, ALU.mult)
+        cast_scalar(0, 2)
+        cast_scalar(0, 0)
+        quantise(0, 2 * HALF, grouped[0, 2][:])
+        quantise(0, 0 * HALF, grouped[0, 0][:])
+        x_picked = pick_words(x_table, "x_picked", 1)
+        nc.vector.tensor_copy(e_scale[:], e_scale_table[:].indirect(offsets[:]))
+        inv_col = held.tile([P, BLOCKS], F32, name="inv_col")
+        root = held.tile([P, BLOCKS], F32, name="root")
+        nc.scalar.copy(inv_col[:], turned[:, 0:S:P])
+        nc.gpsimd.tensor_tensor(root[:], inv_col[:], half[:], ALU.pow)
+        cast_scalar(1, 0)
+        cast_scalar(0, 1)
+        nc.vector.tensor_scalar(grouped[1, 2][:], grouped[1, 0][:], -1.0, None, ALU.mult)
+        quantise(1, 0 * HALF, grouped[1, 0][:])
+        quantise(1, 2 * HALF, grouped[1, 2][:])
+        quantise(0, 1 * HALF, grouped[0, 1][:])
 
-        def quantise(v, slot):
-            cols = slice(slot * P, (slot + 1) * P)
-            nc.vector.quantize_mx(out=codes[v][:, cols].bitcast(FP8X4), scales=scales[v][:, cols], in_=grouped[v][slot][:])
+        units = [(g, a) for g in range(2) for a in range(BLOCKS)]
+        products = {unit: bank(b) for b, unit in enumerate(units)}
 
-        def product_pass(target, v, a, table, start, stop):
+        def product_pass(g, a, table, first, count, column, start, stop):
             if table == "x":
-                words, plane, first = x_picked[a], x_scale[:, a * P : (a + 1) * P], 0
+                words, plane = x_picked[a], x_scale[:, a * P : (a + 1) * P]
             else:
-                words, plane, first = e_picked[a], e_scale[E_PLANE:P, a * P : (a + 1) * P], P
+                words, plane = e_picked[a], e_scale[E_PLANE:P, a * P : (a + 1) * P]
+            cols = slice(first * HALF, (first + count) * HALF)
             nc.tensor.matmul_mx(
-                out=target,
+                out=products[g, a][:, column * HALF : (column + count) * HALF],
                 lhsT=words.bitcast(FP8X4),
                 lhsT_scale=plane,
-                rhs=codes[v][:, first : first + 2 * P].bitcast(FP8X4),
-                rhs_scale=scales[v][:, first : first + 2 * P],
+                rhs=codes[g][:, cols].bitcast(FP8X4),
+                rhs_scale=scales[g][:, cols],
                 start=start,
                 stop=stop,
             )
 
-        products = {}
+        for a in range(BLOCKS):
+            product_pass(0, a, "x", 0, 1, 0, True, False)
+        for a in range(BLOCKS):
+            product_pass(1, a, "x", 0, 1, 0, True, False)
+        for a in range(BLOCKS):
+            product_pass(0, a, "x", 1, 1, 1, False, False)
+        e_picked = pick_words(e_table, "e_picked", 2)
+        for a in range(BLOCKS):
+            product_pass(0, a, "e", 1, 2, 0, False, True)
+        sources = [tile[:].rearrange("p j (c i) -> p c j i", i=4) for tile in raw_last]
+        targets = [tile[:].rearrange("p (c i j) -> p c j i", i=4, j=PACK) for tile in last]
+        nc.scalar.copy(targets[0], sources[0])
+        nc.vector.tensor_copy(targets[1], sources[1])
+        quantise(1, HALF, last[0][:])
+        quantise(1, HALF + P, last[1][:])
+        for a in range(BLOCKS):
+            product_pass(1, a, "e", 2, 1, 1, False, False)
+        for a in range(BLOCKS):
+            product_pass(1, a, "x", 1, 1, 1, False, False)
+            product_pass(1, a, "e", 1, 1, 0, False, True)
+
         squares = {}
+        for unit in units:
+            name = "squares%d_%d" % unit
+            squares[unit] = held.tile([P, 2 * HALF], F32, name=name)
 
-        def open_products(v):
-            for u in range(2):
-                tile = bank(2 * (v % 2) + u)
-                for a in (2 * u, 2 * u + 1):
-                    products[v, a] = tile[:, (a % 2) * 2 * P : (a % 2 + 1) * 2 * P]
+        def square_scalar(g, a):
+            nc.scalar.activation(squares[g, a][:], products[g, a][:], ACT.Square, scale=root[:, a : a + 1])
 
-        def multiply(v):
-            open_products(v)
-            for a in range(BLOCKS):
-                product_pass(products[v, a], v, a, "x", True, False)
-                product_pass(products[v, a], v, a, "e", False, True)
+        sums = {}
 
-        def square(v):
-            for a in range(BLOCKS):
-                squares[v, a] = held.tile([P, 2 * P], F32, name="squares%d_%d" % (v, a))
-                nc.scalar.activation(squares[v, a][:], products[v, a], ACT.Square, scale=root[:, a : a + 1])
+        def add_parts(g, a):
+            sums[g, a] = held.tile([P, HALF], F32, name="sums%d_%d" % (g, a))
+            nc.gpsimd.tensor_tensor(sums[g, a][:], squares[g, a][:, 0:HALF], squares[g, a][:, HALF : 2 * HALF], ALU.add)
 
-        match = {}
+        def square_vector(g, a):
+            plain = held.tile([P, 2 * HALF], F32, name="plain%d_%d" % (g, a), tag="last1", align_bytes=64)
+            nc.vector.tensor_copy(plain[:], products[g, a][:])
+            nc.vector.scalar_tensor_tensor(squares[g, a][:], products[g, a][:], inv_col[:, a : a + 1], plain[:], ALU.mult, ALU.mult)
+
         sixth = [held.tile([P, S], F32, name="sixth%d" % v) for v in range(BLOCKS)]
-        top_sixth = [held.tile([P, 1], F32, name="top%d" % v) for v in range(BLOCKS)]
         gain = [held.tile([P, 1], F32, name="gain%d" % v) for v in range(BLOCKS)]
         weight = [held.tile([P, S], F32, name="weight%d" % v) for v in range(BLOCKS)]
         result = [held.tile([P, S], F32, name="result%d" % v) for v in range(BLOCKS)]
+        match = {v: [] for v in range(BLOCKS)}
+        top_sixth = {}
 
-        def turn(v):
-            match[v] = bank(4 + v)
-            for a in range(BLOCKS):
+        def turn(v, blocks, b):
+            g, first = divmod(v * P, HALF)
+            cols = slice(blocks.start * P, blocks.stop * P)
+            piece = bank(b)[:, cols]
+            for a in blocks:
+                if (g, a) in sums:
+                    nc.tensor.transpose(piece[:, (a - blocks.start) * P : (a - blocks.start + 1) * P], sums[g, a][:, first : first + P], identity[:])
+                    continue
                 for part in range(2):
                     nc.tensor.matmul(
-                        match[v][:, a * P : (a + 1) * P],
-                        squares[v, a][:, part * P : (part + 1) * P],
+                        piece[:, (a - blocks.start) * P : (a - blocks.start + 1) * P],
+                        squares[g, a][:, part * HALF + first : part * HALF + first + P],
                         identity[:],
                         start=(part == 0),
                         stop=(part == 1),
                         is_transpose=True,
                     )
+            match[v].append((cols, piece))
 
-        def best(v):
-            nc.vector.tensor_scalar(sixth[v][:], match[v][:], 1.0 / 6.0, None, ALU.mult, ALU.max, accum_out=top_sixth[v][:])
-            nc.vector.reciprocal(gain[v][:], top_sixth[v][:])
+        def best(v, u):
+            cols, piece = match[v][u]
+            so_far = top_sixth.get(v)
+            top_sixth[v] = held.tile([P, 1], F32, name="top%d_%d" % (v, u))[:]
+            nc.vector.tensor_scalar(sixth[v][:, cols], piece, 1.0 / 6.0, so_far, ALU.mult, ALU.max, accum_out=top_sixth[v])
+            if cols.stop == S:
+                nc.vector.reciprocal(gain[v][:], top_sixth[v])
 
-        def finish(v, pieces):
-            width = S // pieces
-            for u in range(pieces):
-                cols = slice(u * width, (u + 1) * width)
-                nc.scalar.activation(weight[v][:, cols], match[v][:, cols], ACT.Exp, bias=math.log(6.0) - 6.0, scale=gain[v][:])
-                nc.vector.scalar_tensor_tensor(result[v][:, cols], sixth[v][:, cols], gain[v][:], weight[v][:, cols], ALU.mult, ALU.mult)
+        ratio = [held.tile([P, S], F32, name="ratio%d" % v) for v in range(POOL_BLOCKS)]
+
+        def finish(v):
+            if v < POOL_BLOCKS:
+                nc.gpsimd.tensor_scalar(ratio[v][:], sixth[v][:], gain[v][:], 6.0, ALU.mult, ALU.mult)
+            for cols, piece in match[v]:
+                nc.scalar.activation(weight[v][:, cols], piece, ACT.Exp, bias=-6.0, scale=gain[v][:])
+                if v < POOL_BLOCKS:
+                    nc.gpsimd.tensor_tensor(result[v][:, cols], ratio[v][:, cols], weight[v][:, cols], ALU.mult)
+                else:
+                    nc.vector.scalar_tensor_tensor(result[v][:, cols], piece, gain[v][:], weight[v][:, cols], ALU.mult, ALU.mult)
                 nc.sync.dma_start(out[v * P : (v + 1) * P, cols], result[v][:, cols])
 
-        cast_scalar(0, 0, 0, 1.0)
-        cast_scalar(0, 2, 0, -1.0)
-        cast_scalar(0, 1, 1, 1.0)
-        for slot in (0, 2, 1):
-            quantise(0, slot)
-        inv_col = held.tile([P, BLOCKS], F32, name="inv_col")
-        root = held.tile([P, BLOCKS], F32, name="root")
-        nc.scalar.copy(inv_col[:], turned[:, 0:S:P])
-        nc.gpsimd.tensor_tensor(root[:], inv_col[:], half[:], ALU.pow)
-
-        open_products(0)
+        for a in range(BLOCKS - 1):
+            square_scalar(0, a)
+        square_vector(0, BLOCKS - 1)
         for a in range(BLOCKS):
-            product_pass(products[0, a], 0, a, "x", a % 2 == 0, False)
-        e_picked = pick_words(e_table, "e_picked")
-        for a in range(BLOCKS):
-            product_pass(products[0, a], 0, a, "e", False, a % 2 == 1)
-        cast_scalar(1, 0, 0, 1.0)
-        square(0)
-        for v in range(1, BLOCKS):
-            if v > 1:
-                cast_vector(v, 0, 0)
-            negate_vector(v)
-            quantise(v, 0)
-            quantise(v, 2)
-            cast_vector(v, 1, 1)
-            quantise(v, 1)
-            multiply(v)
-            turn(v - 1)
-            square(v)
-        turn(BLOCKS - 1)
-        for v in range(BLOCKS):
-            best(v)
-        for v in range(BLOCKS):
-            finish(v, 2 if v == BLOCKS - 1 else 1)
+            square_scalar(1, a)
+        for g, a in ((0, 0), (0, 1), (1, 0)):
+            add_parts(g, a)
+        turn(0, range(0, 4), 3)
+        turn(1, range(0, 4), 4)
+        turn(2, range(0, 3), 0)
+        turn(2, range(3, 4), 2)
+        turn(3, range(0, 4), 1)
+        best(0, 0)
+        best(1, 0)
+        best(2, 0)
+        best(2, 1)
+        best(3, 0)
+        for v in range(BLOCKS - 1):
+            finish(v)
+        v = BLOCKS - 1
+        for cols in (slice(0, 3 * P), slice(3 * P, S)):
+            nc.scalar.activation(weight[v][:, cols], match[v][0][1][:, cols], ACT.Exp, bias=math.log(6.0) - 6.0, scale=gain[v][:])
+            nc.vector.scalar_tensor_tensor(result[v][:, cols], sixth[v][:, cols], gain[v][:], weight[v][:, cols], ALU.mult, ALU.mult)
+            nc.sync.dma_start(out[v * P : (v + 1) * P, cols], result[v][:, cols])

@@ -1,4 +1,3 @@
-import math
 from contextlib import ExitStack
 
 import concourse.mybir as mybir
@@ -187,40 +186,42 @@ def tile_picked_ymrf_steep_p_kernel(tc, x_words, x_scales, e_words, e_scales, hr
             nc.gpsimd.tensor_tensor(sums[g, a][:], squares[g, a][:, 0:HALF], squares[g, a][:, HALF : 2 * HALF], ALU.add)
 
         def square_vector(g, a):
-            plain = held.tile([P, 2 * HALF], F32, name="plain%d_%d" % (g, a), tag="last1", align_bytes=64)
+            plain = held.tile([P, 2 * HALF], F32, name="plain%d_%d" % (g, a), tag="last0", align_bytes=64)
             nc.vector.tensor_copy(plain[:], products[g, a][:])
             nc.vector.scalar_tensor_tensor(squares[g, a][:], products[g, a][:], inv_col[:, a : a + 1], plain[:], ALU.mult, ALU.mult)
 
         sixth = [held.tile([P, S], F32, name="sixth%d" % v) for v in range(BLOCKS)]
         gain = [held.tile([P, 1], F32, name="gain%d" % v) for v in range(BLOCKS)]
         weight = [held.tile([P, S], F32, name="weight%d" % v) for v in range(BLOCKS)]
-        result = [held.tile([P, S], F32, name="result%d" % v) for v in range(BLOCKS)]
+        result = {}
         match = {v: [] for v in range(BLOCKS)}
         top_sixth = {}
 
-        def turn(v, blocks, b):
-            g, first = divmod(v * P, HALF)
+        def open_match(v, blocks, b):
             cols = slice(blocks.start * P, blocks.stop * P)
-            piece = bank(b)[:, cols]
-            for a in blocks:
-                if (g, a) in sums:
-                    nc.tensor.transpose(piece[:, (a - blocks.start) * P : (a - blocks.start + 1) * P], sums[g, a][:, first : first + P], identity[:])
-                    continue
-                for part in range(2):
-                    nc.tensor.matmul(
-                        piece[:, (a - blocks.start) * P : (a - blocks.start + 1) * P],
-                        squares[g, a][:, part * HALF + first : part * HALF + first + P],
-                        identity[:],
-                        start=(part == 0),
-                        stop=(part == 1),
-                        is_transpose=True,
-                    )
-            match[v].append((cols, piece))
+            match[v].append((cols, bank(b)[:, cols]))
+
+        def turn(v, a):
+            g, first = divmod(v * P, HALF)
+            cols, piece = [entry for entry in match[v] if entry[0].start <= a * P < entry[0].stop][0]
+            target = piece[:, a * P - cols.start : (a + 1) * P - cols.start]
+            if (g, a) in sums:
+                nc.tensor.transpose(target, sums[g, a][:, first : first + P], identity[:])
+                return
+            for part in range(2):
+                nc.tensor.matmul(
+                    target,
+                    squares[g, a][:, part * HALF + first : part * HALF + first + P],
+                    identity[:],
+                    start=(part == 0),
+                    stop=(part == 1),
+                    is_transpose=True,
+                )
 
         def best(v, u):
             cols, piece = match[v][u]
             so_far = top_sixth.get(v)
-            top_sixth[v] = held.tile([P, 1], F32, name="top%d_%d" % (v, u))[:]
+            top_sixth[v] = held.tile([P, 1], F32, name="top%d_%d" % (v, u), tag="top%d_%d" % (v, u))[:]
             nc.vector.tensor_scalar(sixth[v][:, cols], piece, 1.0 / 6.0, so_far, ALU.mult, ALU.max, accum_out=top_sixth[v])
             if cols.stop == S:
                 nc.vector.reciprocal(gain[v][:], top_sixth[v])
@@ -228,6 +229,7 @@ def tile_picked_ymrf_steep_p_kernel(tc, x_words, x_scales, e_words, e_scales, hr
         ratio = [held.tile([P, S], F32, name="ratio%d" % v) for v in range(POOL_BLOCKS)]
 
         def finish(v):
+            result[v] = held.tile([P, S], F32, name="result%d" % v, tag="top2_1" if v == 1 else "result%d" % v)
             if v < POOL_BLOCKS:
                 nc.gpsimd.tensor_scalar(ratio[v][:], sixth[v][:], gain[v][:], 6.0, ALU.mult, ALU.mult)
             for cols, piece in match[v]:
@@ -238,27 +240,31 @@ def tile_picked_ymrf_steep_p_kernel(tc, x_words, x_scales, e_words, e_scales, hr
                     nc.vector.scalar_tensor_tensor(result[v][:, cols], piece, gain[v][:], weight[v][:, cols], ALU.mult, ALU.mult)
                 nc.sync.dma_start(out[v * P : (v + 1) * P, cols], result[v][:, cols])
 
-        for a in range(BLOCKS - 1):
-            square_scalar(0, a)
-        square_vector(0, BLOCKS - 1)
+        square_scalar(0, 0)
+        square_scalar(0, 1)
+        square_vector(0, 2)
+        square_scalar(0, 3)
         for a in range(BLOCKS):
             square_scalar(1, a)
-        for g, a in ((0, 0), (0, 1), (1, 0)):
+        for g, a in ((0, 0), (1, 0)):
             add_parts(g, a)
-        turn(0, range(0, 4), 3)
-        turn(1, range(0, 4), 4)
-        turn(2, range(0, 3), 0)
-        turn(2, range(3, 4), 2)
-        turn(3, range(0, 4), 1)
+        open_match(0, range(0, 4), 3)
+        open_match(1, range(0, 4), 2)
+        open_match(2, range(0, 2), 0)
+        open_match(2, range(2, 4), 4)
+        open_match(3, range(0, 2), 1)
+        open_match(3, range(2, 4), 5)
+        for v in range(2):
+            for a in range(BLOCKS):
+                turn(v, a)
+        for a in (1, 0, 2, 3):
+            turn(2, a)
+            turn(3, a)
         best(0, 0)
         best(1, 0)
         best(2, 0)
-        best(2, 1)
         best(3, 0)
-        for v in range(BLOCKS - 1):
+        best(2, 1)
+        best(3, 1)
+        for v in range(BLOCKS):
             finish(v)
-        v = BLOCKS - 1
-        for cols in (slice(0, 3 * P), slice(3 * P, S)):
-            nc.scalar.activation(weight[v][:, cols], match[v][0][1][:, cols], ACT.Exp, bias=math.log(6.0) - 6.0, scale=gain[v][:])
-            nc.vector.scalar_tensor_tensor(result[v][:, cols], sixth[v][:, cols], gain[v][:], weight[v][:, cols], ALU.mult, ALU.mult)
-            nc.sync.dma_start(out[v * P : (v + 1) * P, cols], result[v][:, cols])

@@ -41,7 +41,6 @@ def tile_picked_ymrf_steep_p_kernel(tc, x_words, x_scales, e_words, e_scales, hr
         e_scale_table = held.tile([P, T], U8, name="e_scale_table", tag="e_scale_table", align_bytes=64)
         inv_table = held.tile([P, T], F32, name="inv_table", tag="inv_table", align_bytes=64)
         half = held.tile([P, BLOCKS], F32, name="half")
-        warm = held.tile([P, 1], F32, name="warm")
         identity = held.tile([P, P], F32, name="identity")
         raw = {(m, g): held.tile([P, PACK, HALF], F32, name="raw%d_%d" % (m, g), tag="raw%d_%d" % (m, g)) for m, g in ((0, 0), (0, 1), (1, 0))}
         raw_last = [held.tile([P, PACK, P], F32, name="raw_last%d" % u) for u in range(2)]
@@ -73,7 +72,6 @@ def tile_picked_ymrf_steep_p_kernel(tc, x_words, x_scales, e_words, e_scales, hr
         nc.sync.dma_start(e_table[:], e_words[0].rearrange("p n r -> p (n r)").bitcast(I32))
         for u in range(2):
             nc.sync.dma_start(raw_last[u][:], signal_rows[1][:, :, HALF + u * P : HALF + (u + 1) * P])
-        nc.scalar.activation(warm[:], half[:, 0:1], ACT.Exp)
 
         x_scale = held.tile([P, S], U8, name="x_scale", align_bytes=64)
         e_scale = held.tile([P, S], U8, name="e_scale", align_bytes=64)

@@ -180,7 +180,7 @@ def tile_picked_ymrf_steep_p_kernel(tc, x_words, x_scales, e_words, e_scales, hr
         sums = {}
 
         def add_parts(g, a):
-            sums[g, a] = held.tile([P, HALF], F32, name="sums%d_%d" % (g, a))
+            sums[g, a] = held.tile([P, HALF], F32, name="sums%d_%d" % (g, a), tag="last1" if g == 0 else "sums1", align_bytes=64)
             nc.gpsimd.tensor_tensor(sums[g, a][:], squares[g, a][:, 0:HALF], squares[g, a][:, HALF : 2 * HALF], ALU.add)
 
         def square_vector(g, a):

@@ -37,17 +37,17 @@ def tile_picked_ymrf_steep_p_kernel(tc, x_words, x_scales, e_words, e_scales, hr
         offsets = held.tile([P, S // 16], U16, name="offsets")
         x_table = held.tile([P, T], I32, name="x_table", tag="x_table", align_bytes=64)
         e_table = held.tile([P, T], I32, name="e_table", tag="e_table", align_bytes=64)
-        x_scale_table = held.tile([P, T], U8, name="x_scale_table")
-        e_scale_table = held.tile([P, T], U8, name="e_scale_table", tag="e_scale_table", align_bytes=64)
-        inv_table = held.tile([P, T], F32, name="inv_table", tag="inv_table", align_bytes=64)
+        x_scale_table = held.tile([P, T], U8, name="x_scale_table", tag="x_scale_table", align_bytes=64)
+        e_scale_table = held.tile([P, T], U8, name="e_scale_table")
+        inv_table = held.tile([P, T], F32, name="inv_table")
         half = held.tile([P, BLOCKS], F32, name="half")
         identity = held.tile([P, P], F32, name="identity")
-        raw = {(m, g): held.tile([P, PACK, HALF], F32, name="raw%d_%d" % (m, g), tag="raw%d_%d" % (m, g)) for m, g in ((0, 0), (0, 1), (1, 0))}
+        raw = {(m, g): held.tile([P, PACK, HALF], F32, name="raw%d_%d" % (m, g), tag="raw%d_%d" % (m, g))[:] for m, g in ((0, 0), (0, 1), (1, 0))}
         raw_last = [held.tile([P, PACK, P], F32, name="raw_last%d" % u) for u in range(2)]
         signal_rows = [m.rearrange("(p j) t -> p j t", j=PACK) for m in (hr, hi)]
 
         def load_signal(m, g):
-            nc.sync.dma_start(raw[m, g][:], signal_rows[m][:, :, g * HALF : (g + 1) * HALF])
+            nc.sync.dma_start(raw[m, g], signal_rows[m][:, :, g * HALF : (g + 1) * HALF])
 
         nc.gpsimd.memset(x_scale_table[:].bitcast(I32), 0)
         nc.vector.memset(inv_table[:, 0:575].bitcast(I32), 0)
@@ -63,8 +63,8 @@ def tile_picked_ymrf_steep_p_kernel(tc, x_words, x_scales, e_words, e_scales, hr
         nc.sync.dma_start(offsets[:], offs)
         for r in range(4):
             nc.sync.dma_start(x_scale_table[r:P:32, :].bitcast(I32), x_rows[r])
-        nc.sync.dma_start(inv_table[0:1, :], inv[0:1, :])
         nc.sync.dma_start(x_table[:], x_words[0].rearrange("p n r -> p (n r)").bitcast(I32))
+        nc.sync.dma_start(inv_table[0:1, :], inv[0:1, :])
         for r in range(4):
             nc.sync.dma_start(e_scale_table[E_PLANE + r : P : 32, :].bitcast(I32), e_rows[r])
         load_signal(0, 1)
@@ -77,54 +77,65 @@ def tile_picked_ymrf_steep_p_kernel(tc, x_words, x_scales, e_words, e_scales, hr
         e_scale = held.tile([P, S], U8, name="e_scale", align_bytes=64)
         inv_row = held.tile([P, S], F32, name="inv_row")
         nc.vector.tensor_copy(x_scale[:], x_scale_table[:].indirect(offsets[:]))
-        nc.vector.tensor_copy(inv_row[:], inv_table[:].indirect(offsets[:]))
 
         def pick_words(table, name, pieces):
             picked = []
-            count = S // pieces
-            for u in range(pieces):
-                words = held.tile([P, count], U32, name="%s%d" % (name, u), align_bytes=64)
-                nc.vector.tensor_copy(words[:], table[:].bitcast(U32).indirect(offsets[:, u * count // 16 : (u + 1) * count // 16]))
+            for count in pieces:
+                first = len(picked) * P
+                words = held.tile([P, count], U32, name="%s%d" % (name, first), align_bytes=64)
+                nc.vector.tensor_copy(words[:], table[:].bitcast(U32).indirect(offsets[:, first // 16 : (first + count) // 16]))
                 picked.extend([words[:, c : c + P] for c in range(0, count, P)])
             return picked
 
-        turned = bank(7)
-        for a in range(BLOCKS):
-            nc.tensor.transpose(turned[:, a * P : (a + 1) * P], inv_row[:, a * P : (a + 1) * P], identity[:])
-
         slot = PACK * HALF
-        codes = [held.tile([P, 3 * HALF], U32, name="codes%d" % g, align_bytes=64) for g in range(2)]
-        scales = [held.tile([P, 3 * HALF], U8, name="scales%d" % g, tag=("inv_table", "e_scale_table")[g], align_bytes=64) for g in range(2)]
+        hr_codes = [held.tile([P, HALF], U32, name="hr_codes%d" % g, align_bytes=64) for g in range(2)]
+        hr_scales = [held.tile([P, HALF], U8, name="hr_scales%d" % g, tag=("x_scale_table", "hr_scales1")[g], align_bytes=64) for g in range(2)]
+        pair_codes = [held.tile([P, 2 * HALF], U32, name="pair_codes%d" % g, tag=("x_table", "pair_codes1")[g], align_bytes=64) for g in range(2)]
+        pair_scales = [held.tile([P, 2 * HALF], U8, name="pair_scales%d" % g, align_bytes=64) for g in range(2)]
+
+        def operand(g, first, count):
+            if first < HALF:
+                return hr_codes[g][:, first : first + count], hr_scales[g][:, first : first + count]
+            cols = slice(first - HALF, first - HALF + count)
+            return pair_codes[g][:, cols], pair_scales[g][:, cols]
+
         grouped = {(g, s): held.tile([P, slot], BF16, name="grouped%d_%d" % (g, s), align_bytes=64) for g in range(2) for s in range(3) if (g, s) != (1, 1)}
         last = [held.tile([P, slot // 2], BF16, name="last%d" % u, tag="last%d" % u, align_bytes=64) for u in range(2)]
 
         def views(g, s):
             return (
                 grouped[g, s][:].rearrange("p (c i j) -> p c j i", i=4, j=PACK),
-                raw[s % 2, g][:].rearrange("p j (c i) -> p c j i", i=4),
+                raw[s % 2, g].rearrange("p j (c i) -> p c j i", i=4),
             )
 
         def cast_scalar(g, s):
             target, source = views(g, s)
             nc.scalar.activation(target, source, ACT.Copy, scale=-1.0 if s == 2 else 1.0)
 
-        def quantise(g, first, values):
-            cols = slice(first, first + values.shape[1] // PACK)
-            nc.vector.quantize_mx(out=codes[g][:, cols].bitcast(FP8X4), scales=scales[g][:, cols], in_=values)
+        def negate(g):
+            nc.vector.tensor_scalar(grouped[g, 2][:], grouped[g, 0][:], -1.0, None, ALU.mult)
 
-        cast_scalar(0, 2)
+        def quantise(g, first, values):
+            words, plane = operand(g, first, values.shape[1] // PACK)
+            nc.vector.quantize_mx(out=words.bitcast(FP8X4), scales=plane, in_=values)
+
         cast_scalar(0, 0)
-        quantise(0, 2 * HALF, grouped[0, 2][:])
+        cast_scalar(0, 2)
+        nc.scalar.activation(inv_row[:], inv_table[:].indirect(offsets[:]), ACT.Copy)
+        turned = bank(7)
+        for a in range(BLOCKS):
+            nc.tensor.transpose(turned[:, a * P : (a + 1) * P], inv_row[:, a * P : (a + 1) * P], identity[:])
         quantise(0, 0 * HALF, grouped[0, 0][:])
-        x_picked = pick_words(x_table, "x_picked", 1)
+        x_picked = pick_words(x_table, "x_picked", [S])
+        quantise(0, 2 * HALF, grouped[0, 2][:])
         nc.vector.tensor_copy(e_scale[:], e_scale_table[:].indirect(offsets[:]))
-        inv_col = held.tile([P, BLOCKS], F32, name="inv_col")
+        cast_scalar(1, 0)
+        cast_scalar(0, 1)
+        inv_col = held.tile([P, BLOCKS], F32, name="inv_col", tag="raw1_0")
         root = held.tile([P, BLOCKS], F32, name="root")
         nc.scalar.copy(inv_col[:], turned[:, 0:S:P])
         nc.gpsimd.tensor_tensor(root[:], inv_col[:], half[:], ALU.pow)
-        cast_scalar(1, 0)
-        cast_scalar(0, 1)
-        nc.vector.tensor_scalar(grouped[1, 2][:], grouped[1, 0][:], -1.0, None, ALU.mult)
+        negate(1)
         quantise(1, 0 * HALF, grouped[1, 0][:])
         quantise(1, 2 * HALF, grouped[1, 2][:])
         quantise(0, 1 * HALF, grouped[0, 1][:])
@@ -137,13 +148,13 @@ def tile_picked_ymrf_steep_p_kernel(tc, x_words, x_scales, e_words, e_scales, hr
                 words, plane = x_picked[a], x_scale[:, a * P : (a + 1) * P]
             else:
                 words, plane = e_picked[a], e_scale[E_PLANE:P, a * P : (a + 1) * P]
-            cols = slice(first * HALF, (first + count) * HALF)
+            moving, moving_plane = operand(g, first * HALF, count * HALF)
             nc.tensor.matmul_mx(
                 out=products[g, a][:, column * HALF : (column + count) * HALF],
                 lhsT=words.bitcast(FP8X4),
                 lhsT_scale=plane,
-                rhs=codes[g][:, cols].bitcast(FP8X4),
-                rhs_scale=scales[g][:, cols],
+                rhs=moving.bitcast(FP8X4),
+                rhs_scale=moving_plane,
                 start=start,
                 stop=stop,
             )
@@ -154,16 +165,19 @@ def tile_picked_ymrf_steep_p_kernel(tc, x_words, x_scales, e_words, e_scales, hr
             product_pass(1, a, "x", 0, 1, 0, True, False)
         for a in range(BLOCKS):
             product_pass(0, a, "x", 1, 1, 1, False, False)
-        e_picked = pick_words(e_table, "e_picked", 2)
+        e_picked = pick_words(e_table, "e_picked", [P, P, 2 * P])
         for a in range(BLOCKS):
             product_pass(0, a, "e", 1, 2, 0, False, True)
+            if a == 1:
+                for b in range(2):
+                    product_pass(1, b, "e", 2, 1, 1, False, False)
         sources = [tile[:].rearrange("p j (c i) -> p c j i", i=4) for tile in raw_last]
         targets = [tile[:].rearrange("p (c i j) -> p c j i", i=4, j=PACK) for tile in last]
         nc.scalar.copy(targets[0], sources[0])
         nc.vector.tensor_copy(targets[1], sources[1])
         quantise(1, HALF, last[0][:])
         quantise(1, HALF + P, last[1][:])
-        for a in range(BLOCKS):
+        for a in range(2, BLOCKS):
             product_pass(1, a, "e", 2, 1, 1, False, False)
         for a in range(BLOCKS):
             product_pass(1, a, "x", 1, 1, 1, False, False)

@@ -23,6 +23,7 @@ BLOCKS = 4
 E_PLANE = 4
 HALF = V // 2
 POOL_BLOCKS = 1
+INV_ROW = 16
 
 
 def tile_picked_ymrf_steep_p_kernel(tc, x_words, x_scales, e_words, e_scales, hr, hi, inv, offs, out):
@@ -64,7 +65,7 @@ def tile_picked_ymrf_steep_p_kernel(tc, x_words, x_scales, e_words, e_scales, hr
         for r in range(4):
             nc.sync.dma_start(x_scale_table[r:P:32, :].bitcast(I32), x_rows[r])
         nc.sync.dma_start(x_table[:], x_words[0].rearrange("p n r -> p (n r)").bitcast(I32))
-        nc.sync.dma_start(inv_table[0:1, :], inv[0:1, :])
+        nc.sync.dma_start(inv_table[INV_ROW : INV_ROW + 1, :], inv[0:1, :])
         for r in range(4):
             nc.sync.dma_start(e_scale_table[E_PLANE + r : P : 32, :].bitcast(I32), e_rows[r])
         load_signal(0, 1)
@@ -133,7 +134,7 @@ def tile_picked_ymrf_steep_p_kernel(tc, x_words, x_scales, e_words, e_scales, hr
         cast_scalar(0, 1)
         inv_col = held.tile([P, BLOCKS], F32, name="inv_col", tag="raw1_0")
         root = held.tile([P, BLOCKS], F32, name="root")
-        nc.scalar.copy(inv_col[:], turned[:, 0:S:P])
+        nc.scalar.copy(inv_col[:], turned[:, INV_ROW:S:P])
         nc.gpsimd.tensor_tensor(root[:], inv_col[:], half[:], ALU.pow)
         negate(1)
         quantise(1, 0 * HALF, grouped[1, 0][:])

@@ -135,7 +135,8 @@ def tile_picked_ymrf_steep_p_kernel(tc, x_words, x_scales, e_words, e_scales, hr
         inv_col = held.tile([P, BLOCKS], F32, name="inv_col", tag="raw1_0")
         root = held.tile([P, BLOCKS], F32, name="root")
         nc.scalar.copy(inv_col[:], turned[:, INV_ROW:S:P])
-        nc.gpsimd.tensor_tensor(root[:], inv_col[:], half[:], ALU.pow)
+        for cols in (slice(0, 1), slice(1, BLOCKS)):
+            nc.gpsimd.tensor_tensor(root[:, cols], inv_col[:, cols], half[:, cols], ALU.pow)
         negate(1)
         quantise(1, 0 * HALF, grouped[1, 0][:])
         quantise(1, 2 * HALF, grouped[1, 2][:])

@@ -30,6 +30,7 @@ def tile_picked_ymrf_steep_p_kernel(tc, x_words, x_scales, e_words, e_scales, hr
     nc = tc.nc
     with ExitStack() as ctx:
         held = ctx.enter_context(tc.tile_pool(name="held", bufs=1))
+        shared = ctx.enter_context(tc.tile_pool(name="shared", bufs=1))
         psum = ctx.enter_context(tc.psum_pool(name="psum", bufs=1))
 
         def bank(b):
@@ -43,7 +44,8 @@ def tile_picked_ymrf_steep_p_kernel(tc, x_words, x_scales, e_words, e_scales, hr
         inv_table = held.tile([P, T], F32, name="inv_table")
         half = held.tile([P, BLOCKS], F32, name="half")
         identity = held.tile([P, P], F32, name="identity")
-        raw = {(m, g): held.tile([P, PACK, HALF], F32, name="raw%d_%d" % (m, g), tag="raw%d_%d" % (m, g))[:] for m, g in ((0, 0), (0, 1), (1, 0))}
+        raw = {(m, g): held.tile([P, PACK, HALF], F32, name="raw%d_%d" % (m, g), tag="raw%d_%d" % (m, g))[:] for m, g in ((0, 0), (0, 1))}
+        raw[1, 0] = shared.tile([P, PACK, HALF], F32, name="raw1_0", align_bytes=64, offset=0)[:]
         raw_last = [held.tile([P, PACK, P], F32, name="raw_last%d" % u) for u in range(2)]
         signal_rows = [m.rearrange("(p j) t -> p j t", j=PACK) for m in (hr, hi)]
 
@@ -92,7 +94,10 @@ def tile_picked_ymrf_steep_p_kernel(tc, x_words, x_scales, e_words, e_scales, hr
         hr_codes = [held.tile([P, HALF], U32, name="hr_codes%d" % g, align_bytes=64) for g in range(2)]
         hr_scales = [held.tile([P, HALF], U8, name="hr_scales%d" % g, tag=("x_scale_table", "hr_scales1")[g], align_bytes=64) for g in range(2)]
         pair_codes = [held.tile([P, 2 * HALF], U32, name="pair_codes%d" % g, tag=("x_table", "pair_codes1")[g], align_bytes=64) for g in range(2)]
-        pair_scales = [held.tile([P, 2 * HALF], U8, name="pair_scales%d" % g, align_bytes=64) for g in range(2)]
+        pair_scales = [
+            held.tile([P, 2 * HALF], U8, name="pair_scales0", align_bytes=64),
+            shared.tile([P, 2 * HALF], U8, name="pair_scales1", align_bytes=64, offset=64),
+        ]
 
         def operand(g, first, count):
             if first < HALF:
@@ -127,20 +132,20 @@ def tile_picked_ymrf_steep_p_kernel(tc, x_words, x_scales, e_words, e_scales, hr
         for a in range(BLOCKS):
             nc.tensor.transpose(turned[:, a * P : (a + 1) * P], inv_row[:, a * P : (a + 1) * P], identity[:])
         quantise(0, 0 * HALF, grouped[0, 0][:])
-        x_picked = pick_words(x_table, "x_picked", [S])
+        x_picked = pick_words(x_table, "x_picked", [2 * P, 2 * P])
         quantise(0, 2 * HALF, grouped[0, 2][:])
         nc.vector.tensor_copy(e_scale[:], e_scale_table[:].indirect(offsets[:]))
         cast_scalar(1, 0)
         cast_scalar(0, 1)
-        inv_col = held.tile([P, BLOCKS], F32, name="inv_col", tag="raw1_0")
+        inv_col = shared.tile([P, BLOCKS], F32, name="inv_col", align_bytes=64, offset=0)
         root = held.tile([P, BLOCKS], F32, name="root")
         nc.scalar.copy(inv_col[:], turned[:, INV_ROW:S:P])
         for cols in (slice(0, 1), slice(1, BLOCKS)):
             nc.gpsimd.tensor_tensor(root[:, cols], inv_col[:, cols], half[:, cols], ALU.pow)
-        negate(1)
         quantise(1, 0 * HALF, grouped[1, 0][:])
-        quantise(1, 2 * HALF, grouped[1, 2][:])
+        negate(1)
         quantise(0, 1 * HALF, grouped[0, 1][:])
+        quantise(1, 2 * HALF, grouped[1, 2][:])
 
         units = [(g, a) for g in range(2) for a in range(BLOCKS)]
         products = {unit: bank(b) for b, unit in enumerate(units)}

@@ -181,7 +181,7 @@ def tile_picked_ymrf_steep_p_kernel(tc, x_words, x_scales, e_words, e_scales, hr
         sources = [tile[:].rearrange("p j (c i) -> p c j i", i=4) for tile in raw_last]
         targets = [tile[:].rearrange("p (c i j) -> p c j i", i=4, j=PACK) for tile in last]
         nc.scalar.copy(targets[0], sources[0])
-        nc.vector.tensor_copy(targets[1], sources[1])
+        nc.vector.tensor_copy(last[1][:].rearrange("p (c j) -> p c j", j=PACK), raw_last[1][:].rearrange("p j c -> p c j"))
         quantise(1, HALF, last[0][:])
         quantise(1, HALF + P, last[1][:])
         for a in range(2, BLOCKS):

@@ -37,16 +37,16 @@ def tile_picked_ymrf_steep_p_kernel(tc, x_words, x_scales, e_words, e_scales, hr
             return psum.tile([P, 512], F32, name="bank%d" % b, tag="bank%d" % b)
 
         offsets = held.tile([P, S // 16], U16, name="offsets")
-        x_table = held.tile([P, T], I32, name="x_table", tag="x_table", align_bytes=64)
-        e_table = held.tile([P, T], I32, name="e_table", tag="e_table", align_bytes=64)
-        x_scale_table = held.tile([P, T], U8, name="x_scale_table", tag="x_scale_table", align_bytes=64)
-        e_scale_table = held.tile([P, T], U8, name="e_scale_table")
-        inv_table = held.tile([P, T], F32, name="inv_table")
+        x_table = held.tile([P, T], I32, name="x_table", tag="x_table", align_bytes=256)
+        e_table = held.tile([P, T], I32, name="e_table", tag="e_table", align_bytes=256)
+        x_scale_table = held.tile([P, T], U8, name="x_scale_table", tag="x_scale_table", align_bytes=256)
+        e_scale_table = held.tile([P, T], U8, name="e_scale_table", align_bytes=256)
+        inv_table = held.tile([P, T], F32, name="inv_table", align_bytes=256)
         half = held.tile([P, BLOCKS], F32, name="half")
         identity = held.tile([P, P], F32, name="identity")
-        raw = {(m, g): held.tile([P, PACK, HALF], F32, name="raw%d_%d" % (m, g), tag="raw%d_%d" % (m, g))[:] for m, g in ((0, 0), (0, 1))}
-        raw[1, 0] = shared.tile([P, PACK, HALF], F32, name="raw1_0", align_bytes=64, offset=0)[:]
-        raw_last = [held.tile([P, PACK, P], F32, name="raw_last%d" % u) for u in range(2)]
+        raw = {(m, g): held.tile([P, PACK, HALF], F32, name="raw%d_%d" % (m, g), tag="raw%d_%d" % (m, g), align_bytes=256)[:] for m, g in ((0, 0), (0, 1))}
+        raw[1, 0] = shared.tile([P, PACK, HALF], F32, name="raw1_0", align_bytes=256, offset=0)[:]
+        raw_last = [held.tile([P, PACK, P], F32, name="raw_last%d" % u, align_bytes=256) for u in range(2)]
         signal_rows = [m.rearrange("(p j) t -> p j t", j=PACK) for m in (hr, hi)]
 
         def load_signal(m, g):
@@ -92,8 +92,8 @@ def tile_picked_ymrf_steep_p_kernel(tc, x_words, x_scales, e_words, e_scales, hr
 
         slot = PACK * HALF
         hr_codes = [held.tile([P, HALF], U32, name="hr_codes%d" % g, align_bytes=64) for g in range(2)]
-        hr_scales = [held.tile([P, HALF], U8, name="hr_scales%d" % g, tag=("x_scale_table", "hr_scales1")[g], align_bytes=64) for g in range(2)]
-        pair_codes = [held.tile([P, 2 * HALF], U32, name="pair_codes%d" % g, tag=("x_table", "pair_codes1")[g], align_bytes=64) for g in range(2)]
+        hr_scales = [held.tile([P, HALF], U8, name="hr_scales%d" % g, tag=("x_scale_table", "hr_scales1")[g], align_bytes=256) for g in range(2)]
+        pair_codes = [held.tile([P, 2 * HALF], U32, name="pair_codes%d" % g, tag=("x_table", "pair_codes1")[g], align_bytes=256) for g in range(2)]
         pair_scales = [
             held.tile([P, 2 * HALF], U8, name="pair_scales0", align_bytes=64),
             shared.tile([P, 2 * HALF], U8, name="pair_scales1", align_bytes=64, offset=64),
@@ -240,7 +240,7 @@ def tile_picked_ymrf_steep_p_kernel(tc, x_words, x_scales, e_words, e_scales, hr
         def best(v, u):
             cols, piece = match[v][u]
             so_far = top_sixth.get(v)
-            top_sixth[v] = held.tile([P, 1], F32, name="top%d_%d" % (v, u), tag="top%d_%d" % (v, u))[:]
+            top_sixth[v] = held.tile([P, 1], F32, name="top%d_%d" % (v, u), tag="top%d_%d" % (v, u), align_bytes=256)[:]
             nc.vector.tensor_scalar(sixth[v][:, cols], piece, 1.0 / 6.0, so_far, ALU.mult, ALU.max, accum_out=top_sixth[v])
             if cols.stop == S:
                 nc.vector.reciprocal(gain[v][:], top_sixth[v])
@@ -248,7 +248,7 @@ def tile_picked_ymrf_steep_p_kernel(tc, x_words, x_scales, e_words, e_scales, hr
         ratio = [held.tile([P, S], F32, name="ratio%d" % v) for v in range(POOL_BLOCKS)]
 
         def finish(v):
-            result[v] = held.tile([P, S], F32, name="result%d" % v, tag="top2_1" if v == 1 else "result%d" % v)
+            result[v] = held.tile([P, S], F32, name="result%d" % v, tag="top2_1" if v == 1 else "result%d" % v, align_bytes=256)
             if v < POOL_BLOCKS:
                 nc.gpsimd.tensor_scalar(ratio[v][:], sixth[v][:], gain[v][:], 6.0, ALU.mult, ALU.mult)
             for cols, piece in match[v]:

from contextlib import ExitStack

import concourse.mybir as mybir
from concourse.masks import make_identity

K, T, S, V = 512, 2048, 512, 512
FLOPS = 4 * 2 * K * V * S
BYTES = 2 * K * T + 2 * (K // 32) * T + 2 * K * V * 4 + T * 4 + 128 * (S // 16) * 2 + V * S * 4

F32 = mybir.dt.float32
BF16 = mybir.dt.bfloat16
I32 = mybir.dt.int32
U32 = mybir.dt.uint32
U16 = mybir.dt.uint16
U8 = mybir.dt.uint8
FP8X4 = mybir.dt.float8_e4m3fn_x4
ALU = mybir.AluOpType
ACT = mybir.ActivationFunctionType

P = 128
PACK = 4
BLOCKS = 4
E_PLANE = 4
HALF = V // 2
POOL_BLOCKS = 1
INV_ROW = 16


def tile_picked_ymrf_steep_p_kernel(tc, x_words, x_scales, e_words, e_scales, hr, hi, inv, offs, out):
    nc = tc.nc
    with ExitStack() as ctx:
        held = ctx.enter_context(tc.tile_pool(name="held", bufs=1))
        shared = ctx.enter_context(tc.tile_pool(name="shared", bufs=1))
        psum = ctx.enter_context(tc.psum_pool(name="psum", bufs=1))

        def bank(b):
            return psum.tile([P, 512], F32, name="bank%d" % b, tag="bank%d" % b)

        offsets = held.tile([P, S // 16], U16, name="offsets")
        x_table = held.tile([P, T], I32, name="x_table", tag="x_table", align_bytes=256)
        e_table = held.tile([P, T], I32, name="e_table", tag="e_table", align_bytes=256)
        x_scale_table = held.tile([P, T], U8, name="x_scale_table", tag="x_scale_table", align_bytes=256)
        e_scale_table = held.tile([P, T], U8, name="e_scale_table", align_bytes=256)
        inv_table = held.tile([P, T], F32, name="inv_table", align_bytes=256)
        half = held.tile([P, BLOCKS], F32, name="half")
        identity = held.tile([P, P], F32, name="identity")
        raw = {(m, g): held.tile([P, PACK, HALF], F32, name="raw%d_%d" % (m, g), tag="raw%d_%d" % (m, g), align_bytes=256)[:] for m, g in ((0, 0), (0, 1))}
        raw[1, 0] = shared.tile([P, PACK, HALF], F32, name="raw1_0", align_bytes=256, offset=0)[:]
        raw_last = [held.tile([P, PACK, P], F32, name="raw_last%d" % u, align_bytes=256) for u in range(2)]
        signal_rows = [m.rearrange("(p j) t -> p j t", j=PACK) for m in (hr, hi)]

        def load_signal(m, g):
            nc.sync.dma_start(raw[m, g], signal_rows[m][:, :, g * HALF : (g + 1) * HALF])

        nc.gpsimd.memset(x_scale_table[:].bitcast(I32), 0)
        nc.vector.memset(inv_table[:, 0:575].bitcast(I32), 0)
        nc.vector.memset(inv_table[:, 575:1152].bitcast(I32), 0)
        nc.gpsimd.memset(inv_table[:, 1152:T].bitcast(I32), 0)
        nc.vector.memset(half[:], 0.5)
        nc.gpsimd.memset(e_scale_table[:].bitcast(I32), 0)
        make_identity(nc, identity[:])

        x_rows = x_scales[0].bitcast(I32).rearrange("(q r) c -> r q c", r=4)
        e_rows = e_scales[0].bitcast(I32).rearrange("(q r) c -> r q c", r=4)
        load_signal(0, 0)
        nc.sync.dma_start(offsets[:], offs)
        for r in range(4):
            nc.sync.dma_start(x_scale_table[r:P:32, :].bitcast(I32), x_rows[r])
        nc.sync.dma_start(x_table[:], x_words[0].rearrange("p n r -> p (n r)").bitcast(I32))
        nc.sync.dma_start(inv_table[INV_ROW : INV_ROW + 1, :], inv[0:1, :])
        for r in range(4):
            nc.sync.dma_start(e_scale_table[E_PLANE + r : P : 32, :].bitcast(I32), e_rows[r])
        load_signal(0, 1)
        load_signal(1, 0)
        nc.sync.dma_start(e_table[:], e_words[0].rearrange("p n r -> p (n r)").bitcast(I32))
        for u in range(2):
            nc.sync.dma_start(raw_last[u][:], signal_rows[1][:, :, HALF + u * P : HALF + (u + 1) * P])

        x_scale = held.tile([P, S], U8, name="x_scale", align_bytes=64)
        e_scale = held.tile([P, S], U8, name="e_scale", align_bytes=64)
        inv_row = held.tile([P, S], F32, name="inv_row")
        nc.vector.tensor_copy(x_scale[:], x_scale_table[:].indirect(offsets[:]))

        def pick_words(table, name, pieces):
            picked = []
            for count in pieces:
                first = len(picked) * P
                words = held.tile([P, count], U32, name="%s%d" % (name, first), align_bytes=64)
                nc.vector.tensor_copy(words[:], table[:].bitcast(U32).indirect(offsets[:, first // 16 : (first + count) // 16]))
                picked.extend([words[:, c : c + P] for c in range(0, count, P)])
            return picked

        slot = PACK * HALF
        hr_codes = [held.tile([P, HALF], U32, name="hr_codes%d" % g, align_bytes=64) for g in range(2)]
        hr_scales = [held.tile([P, HALF], U8, name="hr_scales%d" % g, tag=("x_scale_table", "hr_scales1")[g], align_bytes=256) for g in range(2)]
        pair_codes = [held.tile([P, 2 * HALF], U32, name="pair_codes%d" % g, tag=("x_table", "pair_codes1")[g], align_bytes=256) for g in range(2)]
        pair_scales = [
            held.tile([P, 2 * HALF], U8, name="pair_scales0", align_bytes=64),
            shared.tile([P, 2 * HALF], U8, name="pair_scales1", align_bytes=64, offset=64),
        ]

        def operand(g, first, count):
            if first < HALF:
                return hr_codes[g][:, first : first + count], hr_scales[g][:, first : first + count]
            cols = slice(first - HALF, first - HALF + count)
            return pair_codes[g][:, cols], pair_scales[g][:, cols]

        grouped = {(g, s): held.tile([P, slot], BF16, name="grouped%d_%d" % (g, s), align_bytes=64) for g in range(2) for s in range(3) if (g, s) != (1, 1)}
        last = [held.tile([P, slot // 2], BF16, name="last%d" % u, tag="last%d" % u, align_bytes=64) for u in range(2)]

        def views(g, s):
            return (
                grouped[g, s][:].rearrange("p (c i j) -> p c j i", i=4, j=PACK),
                raw[s % 2, g].rearrange("p j (c i) -> p c j i", i=4),
            )

        def cast_scalar(g, s):
            target, source = views(g, s)
            nc.scalar.activation(target, source, ACT.Copy, scale=-1.0 if s == 2 else 1.0)

        def negate(g):
            nc.vector.tensor_scalar(grouped[g, 2][:], grouped[g, 0][:], -1.0, None, ALU.mult)

        def quantise(g, first, values):
            words, plane = operand(g, first, values.shape[1] // PACK)
            nc.vector.quantize_mx(out=words.bitcast(FP8X4), scales=plane, in_=values)

        cast_scalar(0, 0)
        cast_scalar(0, 2)
        nc.scalar.activation(inv_row[:], inv_table[:].indirect(offsets[:]), ACT.Copy)
        turned = bank(7)
        for a in range(BLOCKS):
            nc.tensor.transpose(turned[:, a * P : (a + 1) * P], inv_row[:, a * P : (a + 1) * P], identity[:])
        quantise(0, 0 * HALF, grouped[0, 0][:])
        x_picked = pick_words(x_table, "x_picked", [2 * P, 2 * P])
        quantise(0, 2 * HALF, grouped[0, 2][:])
        nc.vector.tensor_copy(e_scale[:], e_scale_table[:].indirect(offsets[:]))
        cast_scalar(1, 0)
        cast_scalar(0, 1)
        inv_col = shared.tile([P, BLOCKS], F32, name="inv_col", align_bytes=64, offset=0)
        root = held.tile([P, BLOCKS], F32, name="root")
        nc.scalar.copy(inv_col[:], turned[:, INV_ROW:S:P])
        for cols in (slice(0, 1), slice(1, BLOCKS)):
            nc.gpsimd.tensor_tensor(root[:, cols], inv_col[:, cols], half[:, cols], ALU.pow)
        quantise(1, 0 * HALF, grouped[1, 0][:])
        negate(1)
        quantise(0, 1 * HALF, grouped[0, 1][:])
        quantise(1, 2 * HALF, grouped[1, 2][:])

        units = [(g, a) for g in range(2) for a in range(BLOCKS)]
        products = {unit: bank(b) for b, unit in enumerate(units)}

        def product_pass(g, a, table, first, count, column, start, stop):
            if table == "x":
                words, plane = x_picked[a], x_scale[:, a * P : (a + 1) * P]
            else:
                words, plane = e_picked[a], e_scale[E_PLANE:P, a * P : (a + 1) * P]
            moving, moving_plane = operand(g, first * HALF, count * HALF)
            nc.tensor.matmul_mx(
                out=products[g, a][:, column * HALF : (column + count) * HALF],
                lhsT=words.bitcast(FP8X4),
                lhsT_scale=plane,
                rhs=moving.bitcast(FP8X4),
                rhs_scale=moving_plane,
                start=start,
                stop=stop,
            )

        for a in range(BLOCKS):
            product_pass(0, a, "x", 0, 1, 0, True, False)
        for a in range(BLOCKS):
            product_pass(1, a, "x", 0, 1, 0, True, False)
        for a in range(BLOCKS):
            product_pass(0, a, "x", 1, 1, 1, False, False)
        e_picked = pick_words(e_table, "e_picked", [P, P, 2 * P])
        for a in range(BLOCKS):
            product_pass(0, a, "e", 1, 2, 0, False, True)
            if a == 1:
                for b in range(2):
                    product_pass(1, b, "e", 2, 1, 1, False, False)
        sources = [tile[:].rearrange("p j (c i) -> p c j i", i=4) for tile in raw_last]
        targets = [tile[:].rearrange("p (c i j) -> p c j i", i=4, j=PACK) for tile in last]
        nc.scalar.copy(targets[0], sources[0])
        nc.vector.tensor_copy(last[1][:].rearrange("p (c j) -> p c j", j=PACK), raw_last[1][:].rearrange("p j c -> p c j"))
        quantise(1, HALF, last[0][:])
        quantise(1, HALF + P, last[1][:])
        for a in range(2, BLOCKS):
            product_pass(1, a, "e", 2, 1, 1, False, False)
        for a in range(BLOCKS):
            product_pass(1, a, "x", 1, 1, 1, False, False)
            product_pass(1, a, "e", 1, 1, 0, False, True)

        squares = {}
        for unit in units:
            name = "squares%d_%d" % unit
            squares[unit] = held.tile([P, 2 * HALF], F32, name=name)

        def square_scalar(g, a):
            nc.scalar.activation(squares[g, a][:], products[g, a][:], ACT.Square, scale=root[:, a : a + 1])

        sums = {}

        def add_parts(g, a):
            sums[g, a] = held.tile([P, HALF], F32, name="sums%d_%d" % (g, a), tag="last1" if g == 0 else "sums1", align_bytes=64)
            nc.gpsimd.tensor_tensor(sums[g, a][:], squares[g, a][:, 0:HALF], squares[g, a][:, HALF : 2 * HALF], ALU.add)

        def square_vector(g, a):
            plain = held.tile([P, 2 * HALF], F32, name="plain%d_%d" % (g, a), tag="last0", align_bytes=64)
            nc.vector.tensor_copy(plain[:], products[g, a][:])
            nc.vector.scalar_tensor_tensor(squares[g, a][:], products[g, a][:], inv_col[:, a : a + 1], plain[:], ALU.mult, ALU.mult)

        sixth = [held.tile([P, S], F32, name="sixth%d" % v) for v in range(BLOCKS)]
        gain = [held.tile([P, 1], F32, name="gain%d" % v) for v in range(BLOCKS)]
        weight = [held.tile([P, S], F32, name="weight%d" % v) for v in range(BLOCKS)]
        result = {}
        match = {v: [] for v in range(BLOCKS)}
        top_sixth = {}

        def open_match(v, blocks, b):
            cols = slice(blocks.start * P, blocks.stop * P)
            match[v].append((cols, bank(b)[:, cols]))

        def turn(v, a):
            g, first = divmod(v * P, HALF)
            cols, piece = [entry for entry in match[v] if entry[0].start <= a * P < entry[0].stop][0]
            target = piece[:, a * P - cols.start : (a + 1) * P - cols.start]
            if (g, a) in sums:
                nc.tensor.transpose(target, sums[g, a][:, first : first + P], identity[:])
                return
            for part in range(2):
                nc.tensor.matmul(
                    target,
                    squares[g, a][:, part * HALF + first : part * HALF + first + P],
                    identity[:],
                    start=(part == 0),
                    stop=(part == 1),
                    is_transpose=True,
                )

        def best(v, u):
            cols, piece = match[v][u]
            so_far = top_sixth.get(v)
            top_sixth[v] = held.tile([P, 1], F32, name="top%d_%d" % (v, u), tag="top%d_%d" % (v, u), align_bytes=256)[:]
            nc.vector.tensor_scalar(sixth[v][:, cols], piece, 1.0 / 6.0, so_far, ALU.mult, ALU.max, accum_out=top_sixth[v])
            if cols.stop == S:
                nc.vector.reciprocal(gain[v][:], top_sixth[v])

        ratio = [held.tile([P, S], F32, name="ratio%d" % v) for v in range(POOL_BLOCKS)]

        def finish(v):
            result[v] = held.tile([P, S], F32, name="result%d" % v, tag="top2_1" if v == 1 else "result%d" % v, align_bytes=256)
            if v < POOL_BLOCKS:
                nc.gpsimd.tensor_scalar(ratio[v][:], sixth[v][:], gain[v][:], 6.0, ALU.mult, ALU.mult)
            for cols, piece in match[v]:
                nc.scalar.activation(weight[v][:, cols], piece, ACT.Exp, bias=-6.0, scale=gain[v][:])
                if v < POOL_BLOCKS:
                    nc.gpsimd.tensor_tensor(result[v][:, cols], ratio[v][:, cols], weight[v][:, cols], ALU.mult)
                else:
                    nc.vector.scalar_tensor_tensor(result[v][:, cols], piece, gain[v][:], weight[v][:, cols], ALU.mult, ALU.mult)
                nc.sync.dma_start(out[v * P : (v + 1) * P, cols], result[v][:, cols])

        square_scalar(0, 0)
        square_scalar(0, 1)
        square_vector(0, 2)
        square_scalar(0, 3)
        for a in range(BLOCKS):
            square_scalar(1, a)
        for g, a in ((0, 0), (1, 0)):
            add_parts(g, a)
        open_match(0, range(0, 4), 3)
        open_match(1, range(0, 4), 2)
        open_match(2, range(0, 2), 0)
        open_match(2, range(2, 4), 4)
        open_match(3, range(0, 2), 1)
        open_match(3, range(2, 4), 5)
        for v in range(2):
            for a in range(BLOCKS):
                turn(v, a)
        for a in (1, 0, 2, 3):
            turn(2, a)
            turn(3, a)
        best(0, 0)
        best(1, 0)
        best(2, 0)
        best(3, 0)
        best(2, 1)
        best(3, 1)
        for v in range(BLOCKS):
            finish(v)
